import numpy as np, ml_dtypes
CORES = [78,86,94,102,110,118]
N = 6
import mx_ref
BF = ml_dtypes.bfloat16
def f(rng, *shape):
    return mx_ref.flush((rng.standard_normal(shape, dtype=np.float32) * np.exp2(rng.integers(-2, 3, shape[:-1] + (1,)))).astype(BF))
def wide(rng, *shape, cols=0):
    v = rng.standard_normal(shape, dtype=np.float32) * np.exp2(rng.integers(-12, 13, shape)).astype(np.float32)
    if cols: v *= np.repeat(np.exp2(rng.integers(-cols, cols + 1, shape[:-2] + (1, shape[-1] // 4))) * (rng.random(shape[:-2] + (1, shape[-1] // 4)) > 0.0625), 4, axis=-1).astype(np.float32)
    return mx_ref.flush(v.astype(BF))
T, CAPP, O = 256, 64, 3
def scores(us, x):
    return mx_ref.matmul(mx_ref.quantize(us), mx_ref.quantize(x))[:8] + np.float32(0.0)
def winners(us, x):
    return np.argmax(np.stack([scores(us[s], x[s]) for s in range(N)]), axis=0)
def fill(rng, n, tot, most):
    n = np.array(n)
    while n.sum() < tot:
        q = rng.integers(0, N)
        if n[q] < most[q]: n[q] += 1
    return rng.permutation(np.repeat(np.arange(N), n))
def deal(rng, full):
    return np.stack([fill(rng, [CAPP if q in full[g] else 0 for q in range(N)], T, [CAPP] * N) for g in range(8)])
def one(rng):
    g, s = rng.integers(0, 8), rng.integers(0, N)
    return deal(rng, [[s] if i == g else [] for i in range(8)])
def heads(rng):
    u, h = np.zeros((8, 16, 128, 4), np.float32), np.arange(8)
    u[h, :, h] = rng.choice([-1.0, 1.0], (8, 16, 4)) * (0.25 + np.abs(rng.standard_normal((8, 16, 4)))) * np.exp2(rng.integers(-2, 3, (8, 16, 1)))
    return np.repeat(u.reshape(1, 128, 512).astype(BF), N, axis=0)
def plant(rng, x, us, wn, big=4, tie=None, zero=None):
    v = np.abs(x.astype(np.float32)).reshape(N, 8, 16, T, 4)
    v[v < 2.0 ** -24] = 0
    h, b = np.arange(8), np.float32(big)
    a = np.sign(us.astype(np.float32)).reshape(8, 16, 128, 4)[h, :, h][:, :, None]
    win = (wn == np.arange(N)[:, None, None])[:, :, None, :, None]
    neg = (rng.random((8, T)) < 0.125)[:, None, :, None]
    c = np.where(rng.random(v.shape, dtype=np.float32) < 0.5, np.float32(-1), np.float32(1))
    t = (np.where(neg, np.where(win, -a, -4 * b * a), np.where(win, b * a, c)) * v).astype(np.float32)
    s = np.stack([scores(us, t[r].reshape(128, 4 * T).astype(BF)) for r in range(N)])
    won = np.take_along_axis(s, wn[None], axis=0)[0]
    lost = np.where(win[:, :, 0, :, 0], -np.inf, s).max(axis=0)
    bad = (~(won - lost > 0.5 * np.abs(won)))[:, None, :, None]
    t = np.where(bad, np.where(win, b * a, -a) * v, t).astype(np.float32)
    if tie is not None:
        best = np.where(win, t, np.float32(0)).sum(axis=0)
        t = np.where(tie[:, None, :, None] & (wn < np.arange(N)[:, None, None])[:, :, None, :, None], best, t)
    if zero is not None: t[:, :, :, zero] = 0
    return t.reshape(N, 128, 4 * T).astype(BF)
def narrow(rng, x, us, wn):
    v, h = x.astype(np.float32).reshape(N, 8, 16, T, 4), np.arange(8)
    u = np.abs(us.astype(np.float32)).reshape(8, 16, 128, 4)[h, :, h]
    i, b = np.unravel_index(u.reshape(8, 64).argmin(axis=1), (16, 4))
    win = wn == np.arange(N)[:, None, None]
    part = np.where(win[:, :, None, :, None], v, np.float32(0)).sum(axis=0)
    p = np.exp2(np.floor(np.log2((u[:, :, None] * np.abs(part)).sum(axis=(1, 3))) - np.log2(u[h, i, b])[:, None]) - 12)
    z = np.stack([np.where(part[g, i[g], :, b[g]] < 0, -p[g], p[g]) for g in range(8)])
    close = np.repeat((rng.permutation(T) < T // 3)[None], 8, axis=0)
    other = (wn + rng.integers(1, N, (8, T))) % N
    hold = ((rng.random((N, 8, T)) < 0.25) | (other == np.arange(N)[:, None, None])) & ~win & close
    held = hold | (win & close)
    t = np.where(held[:, :, None, :, None], part, v).astype(np.float32)
    d = np.where(hold, rng.choice([-0.125, 0.125], (N, 8, T)), 0.0)
    for k in range(2):
        for g in range(8): t[:, g, i[g], :, b[g]] = np.where(held[:, g], z[g] * (1.5 + d[:, g]), t[:, g, i[g], :, b[g]])
        s = np.stack([scores(us, t[r].reshape(128, 4 * T).astype(BF)) for r in range(N)])
        if k == 0: d = np.where(s == np.take_along_axis(s, wn[None], axis=0), 2 * d, d)
    now = np.argmax(s, axis=0)
    for g in range(8):
        for k in range(T):
            n = np.bincount(now[g], minlength=N)
            q = n.argmax()
            if n[q] <= CAPP: break
            j = rng.permutation(np.flatnonzero((now[g] == q) & (wn[g] != q)))[:n[q] - CAPP]
            now[g, j] = wn[g, j]; close[g, j] = False
    return np.where(close[:, None, :, None], t, v).reshape(N, 128, 4 * T).astype(BF)
def draw(rng, wn, **k):
    us = heads(rng)
    return {"x": plant(rng, f(rng, N, 128, 4 * T), us[0], wn, **k), "us": us, "w": f(rng, N, 128, 512 * O)}
def setup_inputs(rng):
    return draw(rng, one(rng))
def setup_inputs_equal(rng):
    e, p = CAPP - 8, rng.permutation(T)
    far = np.stack([fill(rng, [8] + [0] * (N - 1), T - e, [8] + [CAPP] * (N - 1)) for g in range(8)])
    wn = np.concatenate([np.zeros((8, e), int), far], axis=1)[:, p]
    tie = np.repeat(np.concatenate([np.ones(e, bool), np.arange(T - e) % 2 == 0])[None], 8, axis=0)[:, p]
    return draw(rng, wn, tie=tie, zero=(np.arange(T) < 4)[p])
def setup_inputs_full(rng):
    s, k = int(rng.integers(0, N)), T // CAPP
    return draw(rng, deal(rng, [[s] + [q for q in rng.permutation(N).tolist() if q != s][:k - 1] for g in range(8)]))
def setup_inputs_near(rng):
    wn = one(rng)
    d = draw(rng, wn); d["x"] = narrow(rng, d["x"], d["us"][0], wn); return d
def setup_inputs_spread(rng):
    wn, us = one(rng), heads(rng)
    e = np.exp2(rng.integers(-4, 5, (N, 8, 1, T, 1))) * ((rng.random((N, 8, 1, T, 1)) > 0.0625) | (wn == np.arange(N)[:, None, None])[:, :, None, :, None])
    x = wide(rng, N, 128, 4 * T).astype(np.float32).reshape(N, 8, 16, T, 4) * e.astype(np.float32)
    return {"x": plant(rng, x, us[0], wn, big=256), "us": us, "w": f(rng, N, 128, 512 * O)}
def setup_inputs_stretch(rng):
    L = []
    for g in range(8):
        s, a = rng.integers(0, N), rng.choice([0, T - CAPP, rng.integers(0, T - CAPP + 1)])
        far = fill(rng, [0] * N, T - CAPP, [0 if q == s else CAPP for q in range(N)])
        L.append(np.concatenate([far[:a], np.full(CAPP, s), far[a:]]))
    return draw(rng, np.stack(L))
def check_inputs(d):
    b = []
    for k in ("x", "us", "w"):
        v = np.abs(np.asarray(d[k]).astype(np.float32))
        if not ((v == 0) | ((v >= 2.0 ** -30) & (v <= 2.0 ** 30))).all(): b.append(k)
    if b: return b
    u, h = np.array(d["us"]).astype(np.float32), np.arange(8)
    same = (u == u[:1]).all()
    u = u.reshape(N, 8, 16, 128, 4); u[:, h, :, h] = 0
    if not same or (u != 0).any(): b.append("us")
    wn = winners(d["us"], d["x"])
    if max((wn == s).sum(axis=1).max() for s in range(N)) > CAPP: b.append("x")
    return b
def reference(x, us, w):
    wn = winners(us, x)
    M = []
    for s in range(N):
        v = np.where((wn == s)[:, None, :, None], x[s].astype(np.float32).reshape(8, 16, T, 4), np.float32(0))
        M.append(mx_ref.quantize(np.ascontiguousarray(v.reshape(128, 4 * T).astype(BF))))
    y = np.zeros((N, 128, O * T), np.float32)
    for r in range(N):
        for o in range(O):
            W = mx_ref.quantize(np.ascontiguousarray(w[r][:, 512 * o:512 * o + 512]))
            for s in range(N): y[r][:, T * o:T * o + T] += mx_ref.matmul(W, M[s])
    return {"y": y, "wn": np.repeat(wn.astype(np.float32)[None], N, axis=0)}

@@ -1,0 +1,440 @@
+from concourse.bass import DstId, RemoteDMATransfer
+from concourse.mybir import dt, AluOpType, ActivationFunctionType
+
+NP = 8
+PW = 384
+CAP = 64
+
+SCRATCH = {}
+
+
+def _bufs(dtype, names):
+    for item in names.split():
+        name, width = item.split(":")
+        SCRATCH[name] = ("sbuf", [128, int(width)], dtype)
+
+
+_bufs("bfloat16", "xb:1040 usb:32 usr:512 zt:8192 zb:1024 wf:1536 hb:512 mb:1024 n16:256 mk:256 rst:256")
+_bufs("float8_e4m3fn_x4", "uq:128 xq:256 hq:128 mq:256 wfq:384 wq:3072 lc:320")
+_bufs("uint8", "up:128 xp:256 hp:128 mp:256 wfp:384 wp:3072 lp:320")
+_bufs("int32", "pidx:1 pci:3 oi:16 oj:16")
+_bufs("uint16", "ul:32 offu:16 cl:16 ml:64 ru:64 lst:256")
+_bufs("float32", "ia:32 pcf:4 n4:64 mk4:64 rst4:64 tc65:16 tc64:16 j4:256 im:16 mj:16 c96:96 rk:96")
+_bufs("float32", "sm:256 sc:256 srep:16 sl:96 ga:96 eo:16 xo:32 cop:40 exo:32 bto:32 n1:16 n2:16 zz:16 wd:384 wm:64 ws:64 n3:16")
+_bufs("float32", "m1:48 c1:48 m01:16 m12:16 c2:16 aa:48 ee:96 cs:96 ctp:104 ex:96 bt:96 eb:96 kk:96 ke:96 t48:48 t16:16 x32:32 xt:32 xx:64 xr:64")
+_bufs("float32", "we:96 w48:48 w16:16 x33:32 wt:32 acc:768")
+_bufs("float32", "pw:%d" % (NP * PW))
+for _b in range(8):
+    SCRATCH["ps%d" % _b] = ("psum", [128, 512], "float32")
+
+SEMAPHORES = ["sv", "ss", "st", "sg", "dx", "du", "dwf", "rc", "ls", "dn", "dy"]
+SEMAPHORES += ["dl%d" % _a for _a in range(4)] + ["dw%d" % _a for _a in range(6)] + ["rs%d" % _a for _a in range(6)]
+
+ADD, SUB, MUL, AND = AluOpType.add, AluOpType.subtract, AluOpType.mult, AluOpType.bitwise_and
+MAX, GT, GE, EQ = AluOpType.max, AluOpType.is_gt, AluOpType.is_ge, AluOpType.is_equal
+COPY = ActivationFunctionType.Copy
+
+
+def rank_program(g, core, T, topo):
+    r = T.rank_of(core)
+    if r is None:
+        return
+    N = len(T.cores)
+    others = [s for s in range(N) if s != r]
+    order = [s for s in range(N) if s % 2 == 0] + [s for s in range(N) if s % 2 == 1]
+
+    queues = {"g": g, "v": g.vector, "s": g.scalar, "t": g.tensor, "y": g.sync}
+    V, S, TE, Y = g.vector, g.scalar, g.tensor, g.sync
+    count = {"sv": 0, "ss": 0, "st": 0, "sg": 0}
+    seen = {}
+
+    def wait(q, sem, n):
+        if n > seen.get((q, sem), 0):
+            queues[q].wait_ge(T.sem[sem], n)
+            seen[(q, sem)] = n
+
+    def done(sem, ins):
+        ins.then_inc(T.sem[sem], 1)
+        count[sem] += 1
+        return count[sem]
+
+    def v(ins):
+        return done("sv", ins)
+
+    def s_(ins):
+        return done("ss", ins)
+
+    def t_(ins):
+        return done("st", ins)
+
+    def vw(n):
+        wait("v", "sv", n)
+
+    def tt(out, a, b, op):
+        return v(V.tensor_tensor(out, a, b, op))
+
+    def ts(out, a, scalar, op):
+        return v(V.tensor_scalar(out, a, scalar, None, op))
+
+    def scan(out, a, b, op0, op1):
+        return v(V.tensor_tensor_scan(out, a, b, 0.0, op0, op1))
+
+    S.dma_start(T.usb[:, :], T.us[:, 0:32]).then_inc(T.sem.du, 16)
+    Y.dma_start(T.xb[:, 0:1024], T.x[:, :]).then_inc(T.sem.dx, 16)
+
+    def iota(out, pattern, base=0, cm=0, flag=True):
+        if flag:
+            return done("sg", g.iota(out, pattern, base, cm, allow_small_or_imprecise_dtypes=True))
+        return done("sg", g.iota(out, pattern, base, cm))
+
+    i_p = iota(T.pidx[:, :], [[1, 1]], 0, 1, False)
+    i_a = iota(T.ia[:, :], [[4, 8], [0, 4]])
+    i_n16 = iota(T.n16[:, :], [[0, 16], [1, 16]])
+    iota(T.oi[:, :], [[1, 16]], 0, 16, False)
+    iota(T.n4[:, :], [[0, 16], [1, 4]])
+    iota(T.im[:, :], [[64, 16]], -1024)
+    i_j4 = iota(T.j4[:, :], [[4, 256]])
+    i_c0 = iota(T.c96[:, :], [[0, 96]])
+    wait("g", "sg", i_c0)
+    for e, s in enumerate(order):
+        slot = others.index(s) if s != r else N - 1
+        iota(T.c96[:, 16 * e:16 * e + 1], [[1, 1]], CAP * slot - 1)
+
+    wait("v", "sg", i_p)
+    ts(T.pci[:, 1:2], T.pidx[:, :], 3, AND)
+    ts(T.pci[:, 0:1], T.pidx[:, :], 15, AND)
+    a = v(V.tensor_scalar(T.pci[:, 2:3], T.pidx[:, :], 2, 3, AluOpType.logical_shift_right, AND))
+    c_zb = v(V.memset(T.zb[:, :], 0.0))
+    vw(a)
+    a = v(V.tensor_copy(T.pcf[:, 0:3], T.pci[:, :]))
+    c_z0 = v(V.memset(T.zt[:, 0:2048], 0.0))
+    vw(a)
+    wait("v", "sg", i_a)
+    c_ul = ts(T.ul[:, :], T.ia[:, :], T.pcf[:, 1:2], ADD)
+    v(V.memset(T.xb[:, 1024:1040], 0.0))
+    wait("v", "du", 16)
+    vw(c_ul)
+    c_u = v(V.tensor_copy(T.usr[:, 0:256], T.usb[:, 0:32].indirect(T.ul[:, 0:16])))
+    wait("s", "du", 16)
+    wait("s", "sv", c_ul)
+    s_u = s_(S.activation(T.usr[:, 256:512], T.usb[:, 0:32].indirect(T.ul[:, 16:32]), COPY))
+    wait("v", "sg", i_n16)
+    ts(T.rst[:, :], T.n16[:, :], 0.0, GT)
+    wait("s", "sv", c_zb)
+    s_z = [s_(S.activation(T.zt[:, 2048 + 1024 * k:3072 + 1024 * k], T.zb[:, :], COPY)) for k in range(6)]
+    vw(c_u)
+    wait("v", "ss", s_u)
+    v(V.quantize_mx(T.uq[:, :], T.up[:, :], T.usr[:, :]))
+    wait("v", "dx", 16)
+    c_xq = v(V.quantize_mx(T.xq[:, :], T.xp[:, :], T.xb[:, 0:1024]))
+    c_mk = ts(T.mk[:, :], T.n16[:, :], T.pcf[:, 0:1], EQ)
+
+    place = [0, 2048, 4096, 6144, 0, 2048]
+
+    def load_w(c):
+        o, f = c // 2, 4 * (c % 2)
+        for h in range(f, f + 4):
+            z = place[c] + 512 * (h - f)
+            Y.dma_start(T.zt[16 * h:16 * h + 16, z:z + 512],
+                        T.w[16 * h:16 * h + 16, 512 * o:512 * o + 512]).then_inc(T.sem["dw%d" % c], 16)
+
+    c_w = {}
+
+    def quant_w(c):
+        wait("v", "dw%d" % c, 64)
+        c_w[c] = v(V.quantize_mx(T.wq[:, 512 * c:512 * c + 512], T.wp[:, 512 * c:512 * c + 512],
+                                 T.zt[:, place[c]:place[c] + 2048]))
+
+    wait("y", "dx", 16)
+    wait("y", "sv", c_z0)
+    load_w(0)
+    wait("y", "ss", s_z[1])
+    load_w(1)
+    Y.dma_start(T.wf[:, :], T.w[:, :]).then_inc(T.sem.dwf, 16)
+    wait("y", "ss", s_z[3])
+    load_w(2)
+
+    wait("t", "sv", c_xq)
+    p_s = t_(TE.matmul_mx(T.ps0[:, 0:256], T.uq[:, 0:128], T.up[:, 0:128], T.xq[:, 0:256], T.xp[:, 0:256], True, True))
+    wait("v", "st", p_s)
+    vw(c_mk)
+    c_ps0 = tt(T.sm[:, :], T.ps0[:, 0:256], T.mk[:, :], MUL)
+    vw(c_ps0)
+    a = scan(T.sc[:, :], T.rst[:, :], T.sm[:, :], MUL, ADD)
+    vw(a)
+    c_so = v(V.tensor_copy(T.srep[:, 0:16], T.sc[:, 15:256:16]))
+
+    turn = [(r + k) % N for k in range(1, N)]
+    dst_ids, emask = [], None
+    for s in turn:
+        rid, pid, _se = topo.addr(T.cores[s])
+        dst_ids.append(DstId(rid=rid, pnc=pid))
+        m = topo.mask(core, T.cores[s])
+        emask = m if emask is None else emask & m
+    ne = len([b for b in range(16) if emask >> b & 1])
+
+    def send(src, dsts, sem):
+        g.remote_dma_fused([RemoteDMATransfer(dst_ids=dst_ids, dma_engine_mask=emask, remote_sem=T.sem[sem],
+                                              srcs=[src], dsts=dsts)], local_sem=T.sem.ls)
+
+    e0 = order.index(r)
+    wait("g", "sv", c_so)
+    send(T.srep[:, 0:16], [T.sl[:, 16 * e0:16 * e0 + 16] for _s in turn], "rs%d" % r)
+
+    iota(T.xo[:, 16:32], [[0, 16]])
+    iota(T.cop[:, 0:1], [[0, 1]])
+    i_z1 = iota(T.wd[:, 0:64], [[0, 64]])
+    iota(T.ctp[:, 0:1], [[0, 1]])
+    iota(T.x32[:, 16:32], [[0, 16]])
+    iota(T.x33[:, 16:32], [[0, 16]])
+    i_rk = iota(T.rk[:, :], [[1, 2], [2, 3], [0, 16]])
+
+    wait("v", "sg", i_j4)
+    ts(T.oj[:, :], T.oi[:, :], 255, AND)
+    a = ts(T.pcf[:, 3:4], T.pcf[:, 0:1], 4.0, MUL)
+    v(V.memset(T.hb[:, 256:512], 0.0))
+    ts(T.mk4[:, :], T.n4[:, :], T.pcf[:, 2:3], EQ)
+    ts(T.rst4[:, :], T.n4[:, :], 0.0, GT)
+    vw(max(a, c_so))
+    v(V.tensor_copy(T.sl[:, 16 * e0:16 * e0 + 16], T.srep[:, 0:16]))
+    ts(T.tc65[:, :], T.oj[:, :], 65.0, ADD)
+    ts(T.tc64[:, :], T.oj[:, :], 64.0, ADD)
+    c_cst = ts(T.mj[:, :], T.im[:, :], T.pcf[:, 3:4], ADD)
+    quant_w(0)
+    wait("y", "sv", c_w[0])
+    load_w(4)
+    wait("y", "ss", s_z[5])
+    load_w(3)
+    quant_w(1)
+    wait("y", "sv", c_w[1])
+    load_w(5)
+
+    at = {}
+
+    def r01():
+        tt(T.m1[:, :], T.sl[:, 0:48], T.sl[:, 48:96], MAX)
+        return tt(T.c1[:, :], T.sl[:, 48:96], T.sl[:, 0:48], GT)
+
+    def r02():
+        tt(T.m12[:, :], T.m1[:, 16:32], T.m1[:, 32:48], MAX)
+        tt(T.c2[:, :], T.m1[:, 16:32], T.m1[:, 0:16], GT)
+        return tt(T.m01[:, :], T.m1[:, 0:16], T.m1[:, 16:32], MAX)
+
+    def r03():
+        tt(T.aa[:, 0:16], T.m1[:, 0:16], T.m12[:, :], GE)
+        return tt(T.aa[:, 32:48], T.m1[:, 32:48], T.m01[:, :], GT)
+
+    def r04():
+        return tt(T.aa[:, 16:32], T.c2[:, :], T.aa[:, 32:48], GT)
+
+    def r05():
+        return tt(T.ee[:, 48:96], T.aa[:, :], T.c1[:, :], MUL)
+
+    def r06():
+        return tt(T.ee[:, 0:48], T.aa[:, :], T.ee[:, 48:96], SUB)
+
+    def r07():
+        a = scan(T.cs[:, :], T.rst[:, 0:96], T.ee[:, :], MUL, ADD)
+        wait("v", "sg", i_rk)
+        tt(T.eb[:, :], T.ee[:, :], T.c96[:, :], ADD)
+        return a
+
+    def r08():
+        return v(V.transpose(T.ctp[:, 1:97], T.cs[:, :]))
+
+    def r09():
+        return scan(T.ex[:, :], T.ctp[:, 0:96], T.rst[:, 0:96], ADD, MUL)
+
+    def r10():
+        return v(V.transpose(T.bt[:, :], T.ex[:, :]))
+
+    def r11():
+        return tt(T.eb[:, 0:96:16], T.eb[:, 0:96:16], T.bt[:, 15:96:16], ADD)
+
+    def r12():
+        return scan(T.kk[:, :], T.rst[:, 0:96], T.eb[:, :], MUL, ADD)
+
+    def r13():
+        return tt(T.ke[:, :], T.kk[:, :], T.ee[:, :], MUL)
+
+    def r14():
+        return tt(T.t48[:, :], T.ke[:, 0:48], T.ke[:, 48:96], ADD)
+
+    def r15():
+        return tt(T.t16[:, :], T.t48[:, 0:16], T.t48[:, 16:32], ADD)
+
+    def r16():
+        return tt(T.x32[:, 0:16], T.t16[:, :], T.t48[:, 32:48], ADD)
+
+    def r17():
+        return v(V.transpose(T.xt[:, :], T.x32[:, :]))
+
+    def r18():
+        for d in range(2):
+            for h in range(2):
+                a = v(V.tensor_copy(T.xx[:, 32 * d + 16 * h:32 * d + 16 * h + 16], T.xt[:, 16 * d:16 * d + 16]))
+        return a
+
+    def r19():
+        return v(V.transpose(T.xr[:, :], T.xx[:, :]))
+
+    def r20():
+        return v(V.tensor_copy(T.ru[:, :], T.xr[:, :]))
+
+    steps = [r01, r02, r03, r04, r05, r06, r07, r08, r09, r10, r11, r12, r13, r14, r15, r16, r17, r18, r19, r20]
+    own = []
+
+    def fill():
+        k = len(at)
+        if k < len(steps):
+            if k:
+                vw(at[k - 1])
+            at[k] = steps[k]()
+
+    def after(n):
+        own.append(n)
+        if len(own) % 2 == 1 or len(own) > 11:
+            fill()
+        vw(n)
+
+    wait("v", "sg", i_z1)
+    vw(c_cst)
+    c_eo = None
+    for s in reversed(turn):
+        wait("v", "rs%d" % s, ne)
+        e = order.index(s)
+        op = GT if s < r else GE
+        if c_eo is None:
+            c_eo = tt(T.eo[:, :], T.srep[:, 0:16], T.sl[:, 16 * e:16 * e + 16], op)
+        else:
+            k = 16 * turn.index(s)
+            a = tt(T.ga[:, k:k + 16], T.srep[:, 0:16], T.sl[:, 16 * e:16 * e + 16], op)
+            vw(a)
+            c_eo = tt(T.eo[:, :], T.eo[:, :], T.ga[:, k:k + 16], MUL)
+    after(c_eo)
+    c_co = scan(T.xo[:, 0:16], T.rst[:, 0:16], T.eo[:, :], MUL, ADD)
+    c_n1 = tt(T.n1[:, :], T.eo[:, :], T.tc65[:, :], MUL)
+    after(c_co)
+    a = v(V.transpose(T.cop[:, 1:33], T.xo[:, :]))
+    vw(c_n1)
+    c_n2 = tt(T.n2[:, :], T.tc64[:, :], T.n1[:, :], SUB)
+    after(a)
+    a = scan(T.exo[:, :], T.cop[:, 0:32], T.rst[:, 0:32], ADD, MUL)
+    vw(c_n2)
+    tt(T.zz[:, :], T.xo[:, 0:16], T.n2[:, :], ADD)
+    after(a)
+    a = v(V.transpose(T.bto[:, :], T.exo[:, :]))
+    after(a)
+    a = ts(T.offu[:, :], T.zz[:, :], T.bto[:, 15:16], ADD)
+    after(a)
+    a = v(V.tensor_copy(T.wd[:, 0:384].indirect(T.offu[:, 0:16]), T.j4[:, :]))
+    after(a)
+    a = tt(T.wm[:, :], T.wd[:, 0:64], T.mk4[:, :], MUL)
+    after(a)
+    a = scan(T.ws[:, :], T.rst4[:, :], T.wm[:, :], MUL, ADD)
+    after(a)
+    c_cl = ts(T.cl[:, :], T.ws[:, 3:64:4], T.pcf[:, 1:2], ADD)
+    wait("s", "sv", c_cl)
+    wait("s", "dx", 16)
+    s_h = s_(S.activation(T.hb[:, 128:256], T.xb[:, 0:1040].indirect(T.cl[:, 8:16]), COPY))
+    after(c_cl)
+    a = v(V.tensor_copy(T.hb[:, 0:128], T.xb[:, 0:1040].indirect(T.cl[:, 0:8])))
+    c_n3 = tt(T.n3[:, :], T.eo[:, :], T.mj[:, :], MUL)
+    after(a)
+    wait("v", "ss", s_h)
+    c_hq = v(V.quantize_mx(T.hq[:, :], T.hp[:, :], T.hb[:, :]))
+    wait("g", "sv", c_hq)
+    lands = []
+    for s in turn:
+        k = [q for q in range(N) if q != s].index(r)
+        lands.append((CAP * k, CAP * k + CAP))
+    send(T.hq[:, 0:CAP].bitcast(dt.uint8), [T.lc[:, b:e].bitcast(dt.uint8) for b, e in lands], "rc")
+    send(T.hp[:, 0:CAP], [T.lp[:, b:e] for b, e in lands], "rc")
+    for k in range(NP):
+        i_p0 = iota(T.pw[:, PW * k + 320:PW * k + PW], [[0, 64]])
+
+    vw(c_n3)
+    for t in range(4):
+        c_ml = ts(T.ml[:, 16 * t:16 * t + 16], T.n3[:, :], 1024.0 + t, ADD)
+    wait("s", "sv", c_ml)
+    for t in range(4):
+        s_m = s_(S.activation(T.mb[:, t:1024:4], T.xb[:, 0:1040].indirect(T.ml[:, 16 * t:16 * t + 16]), COPY))
+    while len(at) < 7:
+        fill()
+    vw(at[5])
+    a = tt(T.we[:, :], T.ee[:, :], T.rk[:, :], MUL)
+    after(a)
+    a = tt(T.w48[:, :], T.we[:, 0:48], T.we[:, 48:96], ADD)
+    after(a)
+    a = tt(T.w16[:, :], T.w48[:, 0:16], T.w48[:, 16:32], ADD)
+    after(a)
+    a = tt(T.x33[:, 0:16], T.w16[:, :], T.w48[:, 32:48], ADD)
+    after(a)
+    c_wt = v(V.transpose(T.wt[:, :], T.x33[:, :]))
+    while len(at) < len(steps):
+        fill()
+    c_ru = at[len(steps) - 1]
+    for k in range(4):
+        for b in range(4):
+            q = "y" if b % 2 == 0 else "s"
+            wait(q, "sv", c_ru)
+            queues[q].dma_start(T.lst[32 * b:32 * b + 32, 64 * k:64 * k + 64],
+                                T.ru[32 * k:32 * k + 32, :]).then_inc(T.sem["dl%d" % k], 16)
+    wait("y", "sv", c_wt)
+    for k in range(4):
+        for h in range(2):
+            Y.dma_start(T.wn[2 * k + h:2 * k + h + 1, :],
+                        T.wt[32 * k:32 * k + 16, 16 * h:16 * h + 16]).then_inc(T.sem.dn, 16)
+
+    wait("v", "dwf", 16)
+    v(V.quantize_mx(T.wfq[:, :], T.wfp[:, :], T.wf[:, :]))
+    wait("v", "ss", s_m)
+    c_mq = v(V.quantize_mx(T.mq[:, :], T.mp[:, :], T.mb[:, :]))
+    wait("t", "sv", c_mq)
+    bank_free = [("sv", c_ps0)] + [None] * 7
+    p_m = [t_(TE.matmul_mx(T["ps%d" % (1 + o)][:, 0:256], T.wfq[:, 128 * o:128 * o + 128],
+                           T.wfp[:, 128 * o:128 * o + 128], T.mq[:, 0:256], T.mp[:, 0:256], True, True)) for o in range(3)]
+    for o in range(3):
+        wait("s", "st", p_m[o])
+        bank_free[1 + o] = ("ss", s_(S.activation(T.acc[:, 256 * o:256 * o + 256], T["ps%d" % (1 + o)][:, 0:256], COPY)))
+    for c in range(2, 6):
+        quant_w(c)
+
+    wait("t", "rc", 2 * ne * len(others))
+    wait("v", "sg", i_p0)
+    items = [(o, h) for h in range(5) for o in (0, 1)]
+    items += [(0, 5), (2, 0), (0, 6), (2, 1), (0, 7), (2, 2), (1, 5), (2, 3), (1, 6), (2, 4), (1, 7), (2, 5), (2, 6), (2, 7)]
+    gath, last = [], {}
+    for n, (o, h) in enumerate(items):
+        bank = T["ps%d" % (n % 8)]
+        wait("t", "sv", c_w[2 * o + h // 4])
+        if bank_free[n % 8] is not None:
+            wait("t", *bank_free[n % 8])
+        w = 1024 * o + 128 * h
+        p = t_(TE.matmul_mx(bank[:, 0:320], T.wq[:, w:w + 128], T.wp[:, w:w + 128], T.lc[:, 0:320], T.lp[:, 0:320], True, True))
+        w0 = PW * (n % NP)
+        if n >= NP:
+            wait("s", "sv", gath[n - NP])
+        wait("s", "st", p)
+        c = s_(S.activation(T.pw[:, w0:w0 + 320], bank[:, 0:320], COPY))
+        bank_free[n % 8] = ("ss", c)
+        wait("v", "ss", c)
+        wait("v", "dl%d" % (h // 2), 64)
+        win = T.pw[:, w0:w0 + PW]
+        m = 8 if n >= 22 else 16
+        for f in range(16 // m):
+            if o in last:
+                vw(last[o][f])
+            acc = T.acc[:, 256 * o + 128 * f:256 * o + 128 * f + 16 * m]
+            a = tt(acc, win.indirect(T.lst[:, 32 * h + 8 * f:32 * h + 8 * f + m]), acc, ADD)
+            last[o] = [a, a] if m == 16 else ([a, last[o][1]] if f == 0 else [last[o][0], a])
+            if h == 7:
+                wait("y", "sv", a)
+                Y.dma_start(T.y[:, 256 * o + 128 * f:256 * o + 128 * f + 16 * m], acc).then_inc(T.sem.dy, 16)
+        gath.append(a)
+
+    wait("y", "dy", 64)
+    wait("y", "dn", 128)
+    wait("g", "ls", 3 * ne)
+    for sem in ("sv", "ss", "st", "sg"):
+        wait("g", sem, count[sem])

@@ -1,9 +1,9 @@
 from concourse.bass import DstId, RemoteDMATransfer
 from concourse.mybir import dt, AluOpType, ActivationFunctionType
 
-NP = 8
-PW = 384
 CAP = 64
+PW = 384
+EARLY = 128
 
 SCRATCH = {}
 
@@ -14,25 +14,29 @@ def _bufs(dtype, names):
         SCRATCH[name] = ("sbuf", [128, int(width)], dtype)
 
 
-_bufs("bfloat16", "xb:1040 usb:32 usr:512 zt:8192 zb:1024 wf:1536 hb:512 mb:1024 n16:256 mk:256 rst:256")
-_bufs("float8_e4m3fn_x4", "uq:128 xq:256 hq:128 mq:256 wfq:384 wq:3072 lc:320")
-_bufs("uint8", "up:128 xp:256 hp:128 mp:256 wfp:384 wp:3072 lp:320")
-_bufs("int32", "pidx:1 pci:3 oi:16 oj:16")
-_bufs("uint16", "ul:32 offu:16 cl:16 ml:64 ru:64 lst:256")
-_bufs("float32", "ia:32 pcf:4 n4:64 mk4:64 rst4:64 tc65:16 tc64:16 j4:256 im:16 mj:16 c96:96 rk:96")
-_bufs("float32", "sm:256 sc:256 srep:16 sl:96 ga:96 eo:16 xo:32 cop:40 exo:32 bto:32 n1:16 n2:16 zz:16 wd:384 wm:64 ws:64 n3:16")
-_bufs("float32", "m1:48 c1:48 m01:16 m12:16 c2:16 aa:48 ee:96 cs:96 ctp:104 ex:96 bt:96 eb:96 kk:96 ke:96 t48:48 t16:16 x32:32 xt:32 xx:64 xr:64")
-_bufs("float32", "we:96 w48:48 w16:16 x33:32 wt:32 acc:768")
-_bufs("float32", "pw:%d" % (NP * PW))
+_bufs("bfloat16", "xb:1280 usb:32 usr:512 zt:8192 n16:256 mk:256 rst:256")
+_bufs("float8_e4m3fn_x4", "uq:128 xq:256 wq:3072 lc:448")
+_bufs("uint8", "up:128 xp:256 wp:3072 lp:448")
+_bufs("int32", "pidx:2 pci:6 uli:32 bci:8")
+_bufs("uint16", "ul:32 bc:8 gl:2 offu:16 cl:16 rn:16 lst:128")
+_bufs("float32", "pcf:3 n4:64 mk4:64 cap4:64 tc65:16 tc64:16 j4:256 c96:96 tab:384")
+_bufs("float32", "sm:256 sc:256 sl:96 ga:96 eo:16 xo:32 cop:40 exo:32 bto:32 n1:16 n2:16 zz:16 wd:2240 wm:64 ws:64")
+_bufs("float32", "m1:48 c1:48 xa:48 ya:48 aa:48 ee:96 cs:96 csb:96 ctp:104 ex:96 bt:96 kk:96 ke:96 t48:48 t16:16 x32:32 xt:32")
+_bufs("float32", "xg:32 xr:32 wv:256 acc:768")
+_bufs("float32", "pw:%d" % (24 * PW))
 for _b in range(8):
     SCRATCH["ps%d" % _b] = ("psum", [128, 512], "float32")
 
-SEMAPHORES = ["sv", "ss", "st", "sg", "dx", "du", "dwf", "rc", "ls", "dn", "dy"]
-SEMAPHORES += ["dl%d" % _a for _a in range(4)] + ["dw%d" % _a for _a in range(6)] + ["rs%d" % _a for _a in range(6)]
+SEMAPHORES = ["sv", "ss", "st", "sg", "dx", "du", "ls", "dn", "dy"]
+SEMAPHORES += ["%s%d" % (_n, _a) for _n in ("dw", "rs", "rc") for _a in range(6)]
 
 ADD, SUB, MUL, AND = AluOpType.add, AluOpType.subtract, AluOpType.mult, AluOpType.bitwise_and
-MAX, GT, GE, EQ = AluOpType.max, AluOpType.is_gt, AluOpType.is_ge, AluOpType.is_equal
+MIN, MAX, GT, GE, EQ = AluOpType.min, AluOpType.max, AluOpType.is_gt, AluOpType.is_ge, AluOpType.is_equal
 COPY = ActivationFunctionType.Copy
+
+TILES = "000110101012020212121222"
+ITEMS = [(int(_o), TILES[:_n].count(_o)) for _n, _o in enumerate(TILES)]
+BY_SCALAR = [(1, 0), (2, 0)]
 
 
 def rank_program(g, core, T, topo):
@@ -40,7 +44,6 @@ def rank_program(g, core, T, topo):
     if r is None:
         return
     N = len(T.cores)
-    others = [s for s in range(N) if s != r]
     order = [s for s in range(N) if s % 2 == 0] + [s for s in range(N) if s % 2 == 1]
 
     queues = {"g": g, "v": g.vector, "s": g.scalar, "t": g.tensor, "y": g.sync}
@@ -79,57 +82,63 @@ def rank_program(g, core, T, topo):
     def scan(out, a, b, op0, op1):
         return v(V.tensor_tensor_scan(out, a, b, 0.0, op0, op1))
 
-    S.dma_start(T.usb[:, :], T.us[:, 0:32]).then_inc(T.sem.du, 16)
-    Y.dma_start(T.xb[:, 0:1024], T.x[:, :]).then_inc(T.sem.dx, 16)
+    def copy(out, a):
+        return v(V.tensor_copy(out, a))
+
+    def turn32(out, a):
+        return v(V.transpose(out, a))
 
     def iota(out, pattern, base=0, cm=0, flag=True):
         if flag:
             return done("sg", g.iota(out, pattern, base, cm, allow_small_or_imprecise_dtypes=True))
         return done("sg", g.iota(out, pattern, base, cm))
 
-    i_p = iota(T.pidx[:, :], [[1, 1]], 0, 1, False)
-    i_a = iota(T.ia[:, :], [[4, 8], [0, 4]])
-    i_n16 = iota(T.n16[:, :], [[0, 16], [1, 16]])
-    iota(T.oi[:, :], [[1, 16]], 0, 16, False)
-    iota(T.n4[:, :], [[0, 16], [1, 4]])
-    iota(T.im[:, :], [[64, 16]], -1024)
-    i_j4 = iota(T.j4[:, :], [[4, 256]])
-    i_c0 = iota(T.c96[:, :], [[0, 96]])
-    wait("g", "sg", i_c0)
-    for e, s in enumerate(order):
-        slot = others.index(s) if s != r else N - 1
-        iota(T.c96[:, 16 * e:16 * e + 1], [[1, 1]], CAP * slot - 1)
+    S.dma_start(T.usb[:, :], T.us[:, 0:32]).then_inc(T.sem.du, 16)
+    Y.dma_start(T.xb[:, 0:1024], T.x[:, :]).then_inc(T.sem.dx, 16)
 
+    i_ul = iota(T.uli[:, :], [[1, 4], [4, 8]], 0, 0, False)
+    i_p = iota(T.pidx[:, :], [[0, 2]], 0, 1, False)
+    i_n16 = iota(T.n16[:, :], [[0, 16], [1, 16]])
+    iota(T.n4[:, :], [[0, 16], [1, 4]])
+    i_bc = iota(T.bci[:, :], [[16, 8]], 15, 0, False)
+
+    def zeros(b, e):
+        return v(V.memset(T.zt[:, b:e], 0.0))
+
+    def zeros_s(b, e):
+        for k in range(b, e, 512):
+            a = s_(S.activation(T.zt[:, k:k + 512], T.zt[:, 7680:8192], COPY))
+        return a
+
+    wait("s", "sv", zeros(7680, 8192))
+    s_z = [zeros_s(1024, 2048)]
+    wait("v", "sg", i_ul)
+    c_ul = copy(T.ul[:, :], T.uli[:, :])
     wait("v", "sg", i_p)
-    ts(T.pci[:, 1:2], T.pidx[:, :], 3, AND)
-    ts(T.pci[:, 0:1], T.pidx[:, :], 15, AND)
-    a = v(V.tensor_scalar(T.pci[:, 2:3], T.pidx[:, :], 2, 3, AluOpType.logical_shift_right, AND))
-    c_zb = v(V.memset(T.zb[:, :], 0.0))
+    a = ts(T.pci[:, 0:1], T.pidx[:, 0:1], 15, AND)
+    c_z0 = zeros(0, 1024)
     vw(a)
-    a = v(V.tensor_copy(T.pcf[:, 0:3], T.pci[:, :]))
-    c_z0 = v(V.memset(T.zt[:, 0:2048], 0.0))
+    a = copy(T.pcf[:, 0:1], T.pci[:, 0:1])
+    wait("v", "sg", i_n16)
+    c_rst = ts(T.rst[:, :], T.n16[:, :], 0.0, GT)
     vw(a)
-    wait("v", "sg", i_a)
-    c_ul = ts(T.ul[:, :], T.ia[:, :], T.pcf[:, 1:2], ADD)
-    v(V.memset(T.xb[:, 1024:1040], 0.0))
+    c_mk = ts(T.mk[:, :], T.n16[:, :], T.pcf[:, 0:1], EQ)
     wait("v", "du", 16)
-    vw(c_ul)
-    c_u = v(V.tensor_copy(T.usr[:, 0:256], T.usb[:, 0:32].indirect(T.ul[:, 0:16])))
     wait("s", "du", 16)
     wait("s", "sv", c_ul)
-    s_u = s_(S.activation(T.usr[:, 256:512], T.usb[:, 0:32].indirect(T.ul[:, 16:32]), COPY))
-    wait("v", "sg", i_n16)
-    ts(T.rst[:, :], T.n16[:, :], 0.0, GT)
-    wait("s", "sv", c_zb)
-    s_z = [s_(S.activation(T.zt[:, 2048 + 1024 * k:3072 + 1024 * k], T.zb[:, :], COPY)) for k in range(6)]
+    for t in range(2):
+        c_u = copy(T.usr[:, t:512:4], T.usb[:, :].indirect(T.ul[:, 8 * t:8 * t + 8]))
+        s_u = s_(S.activation(T.usr[:, t + 2:512:4], T.usb[:, :].indirect(T.ul[:, 8 * t + 16:8 * t + 24]), COPY))
+    s_z += [zeros_s(2048, 3072), zeros_s(4096, 6144), zeros_s(6144, 7680)]
+    zeros(3072, 3584)
     vw(c_u)
     wait("v", "ss", s_u)
     v(V.quantize_mx(T.uq[:, :], T.up[:, :], T.usr[:, :]))
     wait("v", "dx", 16)
     c_xq = v(V.quantize_mx(T.xq[:, :], T.xp[:, :], T.xb[:, 0:1024]))
-    c_mk = ts(T.mk[:, :], T.n16[:, :], T.pcf[:, 0:1], EQ)
+    c_z1 = zeros(3584, 4096)
 
-    place = [0, 2048, 4096, 6144, 0, 2048]
+    place = [0, 2048, 0, 2048, 4096, 6144]
 
     def load_w(c):
         o, f = c // 2, 4 * (c % 2)
@@ -140,164 +149,125 @@ def rank_program(g, core, T, topo):
 
     c_w = {}
 
-    def quant_w(c):
+    def quant_w(c, f=0, n=4):
         wait("v", "dw%d" % c, 64)
-        c_w[c] = v(V.quantize_mx(T.wq[:, 512 * c:512 * c + 512], T.wp[:, 512 * c:512 * c + 512],
-                                 T.zt[:, place[c]:place[c] + 2048]))
+        b, e = 512 * c + 128 * f, 512 * c + 128 * (f + n)
+        a = v(V.quantize_mx(T.wq[:, b:e], T.wp[:, b:e], T.zt[:, place[c] + 512 * f:place[c] + 512 * (f + n)]))
+        for k in range(f, f + n):
+            c_w[4 * c + k] = a
+        return a
 
     wait("y", "dx", 16)
     wait("y", "sv", c_z0)
+    wait("y", "ss", s_z[0])
     load_w(0)
+    wait("y", "sv", c_z1)
     wait("y", "ss", s_z[1])
     load_w(1)
-    Y.dma_start(T.wf[:, :], T.w[:, :]).then_inc(T.sem.dwf, 16)
-    wait("y", "ss", s_z[3])
-    load_w(2)
 
     wait("t", "sv", c_xq)
     p_s = t_(TE.matmul_mx(T.ps0[:, 0:256], T.uq[:, 0:128], T.up[:, 0:128], T.xq[:, 0:256], T.xp[:, 0:256], True, True))
     wait("v", "st", p_s)
     vw(c_mk)
     c_ps0 = tt(T.sm[:, :], T.ps0[:, 0:256], T.mk[:, :], MUL)
-    vw(c_ps0)
+    vw(max(c_ps0, c_rst))
     a = scan(T.sc[:, :], T.rst[:, :], T.sm[:, :], MUL, ADD)
     vw(a)
-    c_so = v(V.tensor_copy(T.srep[:, 0:16], T.sc[:, 15:256:16]))
+    e0 = order.index(r)
+    mine = T.sl[:, 16 * e0:16 * e0 + 16]
+    c_so = copy(mine, T.sc[:, 15:256:16])
 
     turn = [(r + k) % N for k in range(1, N)]
-    dst_ids, emask = [], None
+    dst_id, emask = {}, None
     for s in turn:
         rid, pid, _se = topo.addr(T.cores[s])
-        dst_ids.append(DstId(rid=rid, pnc=pid))
+        dst_id[s] = DstId(rid=rid, pnc=pid)
         m = topo.mask(core, T.cores[s])
         emask = m if emask is None else emask & m
     ne = len([b for b in range(16) if emask >> b & 1])
 
-    def send(src, dsts, sem):
-        g.remote_dma_fused([RemoteDMATransfer(dst_ids=dst_ids, dma_engine_mask=emask, remote_sem=T.sem[sem],
+    def send(src, to, dsts, sem):
+        g.remote_dma_fused([RemoteDMATransfer(dst_ids=[dst_id[s] for s in to], dma_engine_mask=emask, remote_sem=T.sem[sem],
                                               srcs=[src], dsts=dsts)], local_sem=T.sem.ls)
 
-    e0 = order.index(r)
     wait("g", "sv", c_so)
-    send(T.srep[:, 0:16], [T.sl[:, 16 * e0:16 * e0 + 16] for _s in turn], "rs%d" % r)
+    send(mine, turn, [mine for _s in turn], "rs%d" % r)
 
     iota(T.xo[:, 16:32], [[0, 16]])
     iota(T.cop[:, 0:1], [[0, 1]])
-    i_z1 = iota(T.wd[:, 0:64], [[0, 64]])
+    iota(T.tc65[:, :], [[1, 16]], CAP + 1, 16)
+    i_z1 = iota(T.tc64[:, :], [[1, 16]], CAP, 16)
+    iota(T.wd[:, 0:64], [[0, 64]])
+    iota(T.cap4[:, :], [[0, 16], [2048, 4]])
+    i_j4 = iota(T.j4[:, :], [[4, 256]])
     iota(T.ctp[:, 0:1], [[0, 1]])
-    iota(T.x32[:, 16:32], [[0, 16]])
-    iota(T.x33[:, 16:32], [[0, 16]])
-    i_rk = iota(T.rk[:, :], [[1, 2], [2, 3], [0, 16]])
+    for e, s in enumerate(order):
+        i_c = iota(T.c96[:, 16 * e:16 * e + 16], [[0, 16]], CAP * ((r - s) % N) - 1)
+    i_tab = iota(T.tab[:, 0:CAP * (r + 1)], [[-1, r + 1], [0, CAP]], r)
+    if r + 1 < N:
+        i_tab = iota(T.tab[:, CAP * (r + 1):PW], [[-1, N - r - 1], [0, CAP]], N - 1)
 
-    wait("v", "sg", i_j4)
-    ts(T.oj[:, :], T.oi[:, :], 255, AND)
-    a = ts(T.pcf[:, 3:4], T.pcf[:, 0:1], 4.0, MUL)
-    v(V.memset(T.hb[:, 256:512], 0.0))
-    ts(T.mk4[:, :], T.n4[:, :], T.pcf[:, 2:3], EQ)
-    ts(T.rst4[:, :], T.n4[:, :], 0.0, GT)
-    vw(max(a, c_so))
-    v(V.tensor_copy(T.sl[:, 16 * e0:16 * e0 + 16], T.srep[:, 0:16]))
-    ts(T.tc65[:, :], T.oj[:, :], 65.0, ADD)
-    ts(T.tc64[:, :], T.oj[:, :], 64.0, ADD)
-    c_cst = ts(T.mj[:, :], T.im[:, :], T.pcf[:, 3:4], ADD)
-    quant_w(0)
-    wait("y", "sv", c_w[0])
-    load_w(4)
-    wait("y", "ss", s_z[5])
+    wait("y", "sv", quant_w(0))
+    load_w(2)
+    wait("v", "sg", i_bc)
+    ts(T.pci[:, 1:2], T.pidx[:, 0:1], 3, AND)
+    v(V.tensor_scalar(T.pci[:, 2:3], T.pidx[:, 0:1], 2, 3, AluOpType.logical_shift_right, AND))
+    a = ts(T.pci[:, 4:6], T.pidx[:, 0:2], 31, AND)
+    copy(T.bc[:, :], T.bci[:, :])
+    vw(a)
+    a = copy(T.pcf[:, 1:3], T.pci[:, 1:3])
+    copy(T.gl[:, :], T.pci[:, 4:6])
+    vw(a)
+    c_cst = ts(T.mk4[:, :], T.n4[:, :], T.pcf[:, 2:3], EQ)
+    wait("y", "sv", quant_w(1))
     load_w(3)
-    quant_w(1)
-    wait("y", "sv", c_w[1])
+    wait("y", "ss", s_z[2])
+    load_w(4)
+    wait("y", "ss", s_z[3])
     load_w(5)
 
+    def need(sem, n, call):
+        wait("v", sem, n)
+        return call()
+
+    steps = [
+        ("m1", [], lambda: tt(T.m1[:, :], T.sl[:, 0:48], T.sl[:, 48:96], MAX)),
+        ("c1", [], lambda: tt(T.c1[:, :], T.sl[:, 48:96], T.sl[:, 0:48], GT)),
+        ("x0", ["m1"], lambda: tt(T.xa[:, 0:32], T.m1[:, 0:32], T.m1[:, 16:48], GE)),
+        ("y1", ["m1"], lambda: tt(T.ya[:, 16:48], T.m1[:, 16:48], T.m1[:, 0:32], GT)),
+        ("x1", ["m1"], lambda: tt(T.xa[:, 32:48], T.m1[:, 32:48], T.m1[:, 0:16], GT)),
+        ("y0", ["m1"], lambda: tt(T.ya[:, 0:16], T.m1[:, 0:16], T.m1[:, 32:48], GE)),
+        ("aa", ["y0"], lambda: tt(T.aa[:, :], T.xa[:, :], T.ya[:, :], MUL)),
+        ("e1", ["aa"], lambda: tt(T.ee[:, 48:96], T.aa[:, :], T.c1[:, :], MUL)),
+        ("e0", ["aa"], lambda: tt(T.ee[:, 0:48], T.aa[:, :], T.c1[:, :], GT)),
+        ("cs", ["e0"], lambda: scan(T.cs[:, :], T.rst[:, 0:96], T.ee[:, :], MUL, ADD)),
+        ("ct", ["cs"], lambda: need("sg", i_c, lambda: turn32(T.ctp[:, 1:97], T.cs[:, :]))),
+        ("cb", ["cs"], lambda: tt(T.csb[:, :], T.cs[:, :], T.c96[:, :], ADD)),
+        ("ex", ["ct"], lambda: scan(T.ex[:, :], T.ctp[:, 0:96], T.rst[:, 0:96], ADD, MUL)),
+        ("bt", ["ex"], lambda: turn32(T.bt[:, :], T.ex[:, :])),
+        ("kk", ["bt"], lambda: tt(T.kk[:, :], T.bt[:, :].indirect(T.bc[:, 0:6]), T.csb[:, :], ADD)),
+        ("ke", ["kk"], lambda: tt(T.ke[:, :], T.kk[:, :], T.ee[:, :], MUL)),
+        ("t3", ["ke"], lambda: tt(T.t48[:, :], T.ke[:, 0:48], T.ke[:, 48:96], ADD)),
+        ("t2", ["t3"], lambda: tt(T.t16[:, :], T.t48[:, 0:16], T.t48[:, 16:32], ADD)),
+        ("r0", ["t2"], lambda: tt(T.x32[:, 0:16], T.t16[:, :], T.t48[:, 32:48], ADD)),
+        ("r1", ["t2"], lambda: tt(T.x32[:, 16:32], T.t16[:, :], T.t48[:, 32:48], ADD)),
+        ("xt", ["r1"], lambda: turn32(T.xt[:, :], T.x32[:, :])),
+        ("rn", ["r0"], lambda: copy(T.rn[:, :], T.x32[:, 0:16])),
+        ("xg", ["xt"], lambda: copy(T.xg[:, :], T.xt[:, :].indirect(T.gl[:, :]))),
+        ("xr", ["xg"], lambda: turn32(T.xr[:, :], T.xg[:, :])),
+    ]
     at = {}
 
-    def r01():
-        tt(T.m1[:, :], T.sl[:, 0:48], T.sl[:, 48:96], MAX)
-        return tt(T.c1[:, :], T.sl[:, 48:96], T.sl[:, 0:48], GT)
-
-    def r02():
-        tt(T.m12[:, :], T.m1[:, 16:32], T.m1[:, 32:48], MAX)
-        tt(T.c2[:, :], T.m1[:, 16:32], T.m1[:, 0:16], GT)
-        return tt(T.m01[:, :], T.m1[:, 0:16], T.m1[:, 16:32], MAX)
-
-    def r03():
-        tt(T.aa[:, 0:16], T.m1[:, 0:16], T.m12[:, :], GE)
-        return tt(T.aa[:, 32:48], T.m1[:, 32:48], T.m01[:, :], GT)
-
-    def r04():
-        return tt(T.aa[:, 16:32], T.c2[:, :], T.aa[:, 32:48], GT)
-
-    def r05():
-        return tt(T.ee[:, 48:96], T.aa[:, :], T.c1[:, :], MUL)
-
-    def r06():
-        return tt(T.ee[:, 0:48], T.aa[:, :], T.ee[:, 48:96], SUB)
-
-    def r07():
-        a = scan(T.cs[:, :], T.rst[:, 0:96], T.ee[:, :], MUL, ADD)
-        wait("v", "sg", i_rk)
-        tt(T.eb[:, :], T.ee[:, :], T.c96[:, :], ADD)
-        return a
-
-    def r08():
-        return v(V.transpose(T.ctp[:, 1:97], T.cs[:, :]))
-
-    def r09():
-        return scan(T.ex[:, :], T.ctp[:, 0:96], T.rst[:, 0:96], ADD, MUL)
-
-    def r10():
-        return v(V.transpose(T.bt[:, :], T.ex[:, :]))
-
-    def r11():
-        return tt(T.eb[:, 0:96:16], T.eb[:, 0:96:16], T.bt[:, 15:96:16], ADD)
-
-    def r12():
-        return scan(T.kk[:, :], T.rst[:, 0:96], T.eb[:, :], MUL, ADD)
-
-    def r13():
-        return tt(T.ke[:, :], T.kk[:, :], T.ee[:, :], MUL)
-
-    def r14():
-        return tt(T.t48[:, :], T.ke[:, 0:48], T.ke[:, 48:96], ADD)
-
-    def r15():
-        return tt(T.t16[:, :], T.t48[:, 0:16], T.t48[:, 16:32], ADD)
-
-    def r16():
-        return tt(T.x32[:, 0:16], T.t16[:, :], T.t48[:, 32:48], ADD)
-
-    def r17():
-        return v(V.transpose(T.xt[:, :], T.x32[:, :]))
-
-    def r18():
-        for d in range(2):
-            for h in range(2):
-                a = v(V.tensor_copy(T.xx[:, 32 * d + 16 * h:32 * d + 16 * h + 16], T.xt[:, 16 * d:16 * d + 16]))
-        return a
-
-    def r19():
-        return v(V.transpose(T.xr[:, :], T.xx[:, :]))
-
-    def r20():
-        return v(V.tensor_copy(T.ru[:, :], T.xr[:, :]))
-
-    steps = [r01, r02, r03, r04, r05, r06, r07, r08, r09, r10, r11, r12, r13, r14, r15, r16, r17, r18, r19, r20]
-    own = []
-
     def fill():
-        k = len(at)
-        if k < len(steps):
-            if k:
-                vw(at[k - 1])
-            at[k] = steps[k]()
+        name, reads, call = steps[len(at)]
+        for x in reads:
+            vw(at[x])
+        at[name] = call()
 
     def after(n):
-        own.append(n)
-        if len(own) % 2 == 1 or len(own) > 11:
-            fill()
+        fill()
         vw(n)
 
-    wait("v", "sg", i_z1)
     vw(c_cst)
     c_eo = None
     for s in reversed(turn):
@@ -305,136 +275,129 @@ def rank_program(g, core, T, topo):
         e = order.index(s)
         op = GT if s < r else GE
         if c_eo is None:
-            c_eo = tt(T.eo[:, :], T.srep[:, 0:16], T.sl[:, 16 * e:16 * e + 16], op)
+            c_eo = tt(T.eo[:, :], mine, T.sl[:, 16 * e:16 * e + 16], op)
         else:
             k = 16 * turn.index(s)
-            a = tt(T.ga[:, k:k + 16], T.srep[:, 0:16], T.sl[:, 16 * e:16 * e + 16], op)
+            a = tt(T.ga[:, k:k + 16], mine, T.sl[:, 16 * e:16 * e + 16], op)
+            if s == turn[0]:
+                fill()
             vw(a)
             c_eo = tt(T.eo[:, :], T.eo[:, :], T.ga[:, k:k + 16], MUL)
+    wait("v", "sg", i_z1)
     after(c_eo)
     c_co = scan(T.xo[:, 0:16], T.rst[:, 0:16], T.eo[:, :], MUL, ADD)
     c_n1 = tt(T.n1[:, :], T.eo[:, :], T.tc65[:, :], MUL)
-    after(c_co)
-    a = v(V.transpose(T.cop[:, 1:33], T.xo[:, :]))
+    vw(c_co)
+    a = turn32(T.cop[:, 1:33], T.xo[:, :])
     vw(c_n1)
     c_n2 = tt(T.n2[:, :], T.tc64[:, :], T.n1[:, :], SUB)
-    after(a)
+    vw(a)
     a = scan(T.exo[:, :], T.cop[:, 0:32], T.rst[:, 0:32], ADD, MUL)
     vw(c_n2)
-    tt(T.zz[:, :], T.xo[:, 0:16], T.n2[:, :], ADD)
-    after(a)
-    a = v(V.transpose(T.bto[:, :], T.exo[:, :]))
-    after(a)
+    b = tt(T.zz[:, :], T.xo[:, 0:16], T.n2[:, :], ADD)
+    vw(a)
+    a = turn32(T.bto[:, :], T.exo[:, :])
+    after(max(a, b))
     a = ts(T.offu[:, :], T.zz[:, :], T.bto[:, 15:16], ADD)
+    wait("v", "sg", i_j4)
     after(a)
-    a = v(V.tensor_copy(T.wd[:, 0:384].indirect(T.offu[:, 0:16]), T.j4[:, :]))
+    a = copy(T.wd[:, :].indirect(T.offu[:, 0:16]), T.j4[:, :])
     after(a)
     a = tt(T.wm[:, :], T.wd[:, 0:64], T.mk4[:, :], MUL)
     after(a)
-    a = scan(T.ws[:, :], T.rst4[:, :], T.wm[:, :], MUL, ADD)
+    a = scan(T.ws[:, :], T.cap4[:, :], T.wm[:, :], MIN, ADD)
     after(a)
     c_cl = ts(T.cl[:, :], T.ws[:, 3:64:4], T.pcf[:, 1:2], ADD)
     wait("s", "sv", c_cl)
     wait("s", "dx", 16)
-    s_h = s_(S.activation(T.hb[:, 128:256], T.xb[:, 0:1040].indirect(T.cl[:, 8:16]), COPY))
+    s_h = s_(S.activation(T.xb[:, 1152:1280], T.xb[:, 0:1024].indirect(T.cl[:, 8:16]), COPY))
     after(c_cl)
-    a = v(V.tensor_copy(T.hb[:, 0:128], T.xb[:, 0:1040].indirect(T.cl[:, 0:8])))
-    c_n3 = tt(T.n3[:, :], T.eo[:, :], T.mj[:, :], MUL)
+    a = copy(T.xb[:, 1024:1152], T.xb[:, 0:1024].indirect(T.cl[:, 0:8]))
     after(a)
     wait("v", "ss", s_h)
-    c_hq = v(V.quantize_mx(T.hq[:, :], T.hp[:, :], T.hb[:, :]))
+    c_hq = v(V.quantize_mx(T.lc[:, 0:128], T.lp[:, 0:128], T.xb[:, 768:1280]))
+
+    def lands(buf, to):
+        return [buf[:, CAP * (2 + turn.index(s)):CAP * (3 + turn.index(s))] for s in to]
+
     wait("g", "sv", c_hq)
-    lands = []
-    for s in turn:
-        k = [q for q in range(N) if q != s].index(r)
-        lands.append((CAP * k, CAP * k + CAP))
-    send(T.hq[:, 0:CAP].bitcast(dt.uint8), [T.lc[:, b:e].bitcast(dt.uint8) for b, e in lands], "rc")
-    send(T.hp[:, 0:CAP], [T.lp[:, b:e] for b, e in lands], "rc")
-    for k in range(NP):
-        i_p0 = iota(T.pw[:, PW * k + 320:PW * k + PW], [[0, 64]])
+    send(T.lp[:, CAP:2 * CAP], turn[:1], lands(T.lp, turn[:1]), "rc%d" % r)
+    send(T.lc[:, CAP:2 * CAP].bitcast(dt.uint8), turn, [x.bitcast(dt.uint8) for x in lands(T.lc, turn)], "rc%d" % r)
+    send(T.lp[:, CAP:2 * CAP], turn[1:], lands(T.lp, turn[1:]), "rc%d" % r)
 
-    vw(c_n3)
-    for t in range(4):
-        c_ml = ts(T.ml[:, 16 * t:16 * t + 16], T.n3[:, :], 1024.0 + t, ADD)
-    wait("s", "sv", c_ml)
-    for t in range(4):
-        s_m = s_(S.activation(T.mb[:, t:1024:4], T.xb[:, 0:1040].indirect(T.ml[:, 16 * t:16 * t + 16]), COPY))
-    while len(at) < 7:
-        fill()
-    vw(at[5])
-    a = tt(T.we[:, :], T.ee[:, :], T.rk[:, :], MUL)
-    after(a)
-    a = tt(T.w48[:, :], T.we[:, 0:48], T.we[:, 48:96], ADD)
-    after(a)
-    a = tt(T.w16[:, :], T.w48[:, 0:16], T.w48[:, 16:32], ADD)
-    after(a)
-    a = tt(T.x33[:, 0:16], T.w16[:, :], T.w48[:, 32:48], ADD)
-    after(a)
-    c_wt = v(V.transpose(T.wt[:, :], T.x33[:, :]))
+    tiles = [(c, f) for c in (2, 3) for f in range(4)]
     while len(at) < len(steps):
+        if tiles and count["sv"] in [at[x] for x in steps[len(at)][1]]:
+            quant_w(*tiles.pop(0), 1)
         fill()
-    c_ru = at[len(steps) - 1]
+    vw(at["xr"])
     for k in range(4):
-        for b in range(4):
-            q = "y" if b % 2 == 0 else "s"
-            wait(q, "sv", c_ru)
-            queues[q].dma_start(T.lst[32 * b:32 * b + 32, 64 * k:64 * k + 64],
-                                T.ru[32 * k:32 * k + 32, :]).then_inc(T.sem["dl%d" % k], 16)
-    wait("y", "sv", c_wt)
-    for k in range(4):
-        for h in range(2):
-            Y.dma_start(T.wn[2 * k + h:2 * k + h + 1, :],
-                        T.wt[32 * k:32 * k + 16, 16 * h:16 * h + 16]).then_inc(T.sem.dn, 16)
+        a = copy(T.lst[0:32, 32 * k:32 * k + 32], T.xr[32 * k:32 * k + 32, :])
+    quant_w(4)
+    vw(a)
+    for k in range(1, 4):
+        c_lst = copy(T.lst[32 * k:32 * k + 32, :], T.lst[0:32, :])
+    quant_w(5)
 
-    wait("v", "dwf", 16)
-    v(V.quantize_mx(T.wfq[:, :], T.wfp[:, :], T.wf[:, :]))
-    wait("v", "ss", s_m)
-    c_mq = v(V.quantize_mx(T.mq[:, :], T.mp[:, :], T.mb[:, :]))
-    wait("t", "sv", c_mq)
     bank_free = [("sv", c_ps0)] + [None] * 7
-    p_m = [t_(TE.matmul_mx(T["ps%d" % (1 + o)][:, 0:256], T.wfq[:, 128 * o:128 * o + 128],
-                           T.wfp[:, 128 * o:128 * o + 128], T.mq[:, 0:256], T.mp[:, 0:256], True, True)) for o in range(3)]
-    for o in range(3):
-        wait("s", "st", p_m[o])
-        bank_free[1 + o] = ("ss", s_(S.activation(T.acc[:, 256 * o:256 * o + 256], T["ps%d" % (1 + o)][:, 0:256], COPY)))
-    for c in range(2, 6):
-        quant_w(c)
+    made = [0]
 
-    wait("t", "rc", 2 * ne * len(others))
-    wait("v", "sg", i_p0)
-    items = [(o, h) for h in range(5) for o in (0, 1)]
-    items += [(0, 5), (2, 0), (0, 6), (2, 1), (0, 7), (2, 2), (1, 5), (2, 3), (1, 6), (2, 4), (1, 7), (2, 5), (2, 6), (2, 7)]
-    gath, last = [], {}
-    for n, (o, h) in enumerate(items):
-        bank = T["ps%d" % (n % 8)]
-        wait("t", "sv", c_w[2 * o + h // 4])
-        if bank_free[n % 8] is not None:
-            wait("t", *bank_free[n % 8])
-        w = 1024 * o + 128 * h
-        p = t_(TE.matmul_mx(bank[:, 0:320], T.wq[:, w:w + 128], T.wp[:, w:w + 128], T.lc[:, 0:320], T.lp[:, 0:320], True, True))
-        w0 = PW * (n % NP)
-        if n >= NP:
-            wait("s", "sv", gath[n - NP])
+    def product(o, h, b, e):
+        n = made[0] % 8
+        made[0] += 1
+        bank, w = T["ps%d" % n], 1024 * o + 128 * h
+        wait("t", "sv", c_w[8 * o + h])
+        if bank_free[n] is not None:
+            wait("t", *bank_free[n])
+        p = t_(TE.matmul_mx(bank[:, 0:e - b], T.wq[:, w:w + 128], T.wp[:, w:w + 128],
+                            T.lc[:, CAP + b:CAP + e], T.lp[:, CAP + b:CAP + e], True, True))
         wait("s", "st", p)
-        c = s_(S.activation(T.pw[:, w0:w0 + 320], bank[:, 0:320], COPY))
-        bank_free[n % 8] = ("ss", c)
+        w0 = PW * (8 * o + h)
+        bank_free[n] = ("ss", s_(S.activation(T.pw[:, w0 + b:w0 + e], bank[:, 0:e - b], COPY)))
+        return bank_free[n][1]
+
+    wait("t", "sv", c_hq)
+    wait("t", "rc%d" % turn[-1], 2 * ne)
+    for o in range(2):
+        if o == 1:
+            wait("s", "sv", at["rn"])
+            wait("s", "sg", i_tab)
+            wait("y", "ss", s_(S.activation(T.wv[:, :], T.tab[:, :].indirect(T.rn[:, :]), COPY)))
+            for h in range(8):
+                Y.dma_start(T.wn[h:h + 1, :], T.wv[16 * h:16 * h + 1, :]).then_inc(T.sem.dn, 16)
+        for h in range(8):
+            product(o, h, 0, EARLY)
+    for s in turn[:-1]:
+        wait("t", "rc%d" % s, 2 * ne)
+
+    last = {}
+    for n, (o, h) in enumerate(ITEMS):
+        c = product(o, h, EARLY if o < 2 else 0, PW)
+        win = T.pw[:, PW * (8 * o + h):PW * (8 * o + h + 1)]
+        if (o, h) in BY_SCALAR:
+            wait("s", "ss", c)
+            wait("s", "sv", c_lst)
+            a = s_(S.activation(T.acc[:, 256 * o:256 * o + 256], win.indirect(T.lst[:, 16 * h:16 * h + 16]), COPY))
+            last[o] = [("ss", a), ("ss", a)]
+            continue
         wait("v", "ss", c)
-        wait("v", "dl%d" % (h // 2), 64)
-        win = T.pw[:, w0:w0 + PW]
+        vw(c_lst)
         m = 8 if n >= 22 else 16
         for f in range(16 // m):
-            if o in last:
-                vw(last[o][f])
             acc = T.acc[:, 256 * o + 128 * f:256 * o + 128 * f + 16 * m]
-            a = tt(acc, win.indirect(T.lst[:, 32 * h + 8 * f:32 * h + 8 * f + m]), acc, ADD)
+            picked = win.indirect(T.lst[:, 16 * h + 8 * f:16 * h + 8 * f + m])
+            if o in last:
+                wait("v", *last[o][f])
+                a = ("sv", tt(acc, picked, acc, ADD))
+            else:
+                a = ("sv", copy(acc, picked))
             last[o] = [a, a] if m == 16 else ([a, last[o][1]] if f == 0 else [last[o][0], a])
             if h == 7:
-                wait("y", "sv", a)
+                wait("y", *a)
                 Y.dma_start(T.y[:, 256 * o + 128 * f:256 * o + 128 * f + 16 * m], acc).then_inc(T.sem.dy, 16)
-        gath.append(a)
 
     wait("y", "dy", 64)
     wait("y", "dn", 128)
-    wait("g", "ls", 3 * ne)
+    wait("g", "ls", 4 * ne)
     for sem in ("sv", "ss", "st", "sg"):
         wait("g", sem, count[sem])

@@ -3,7 +3,8 @@ from concourse.mybir import dt, AluOpType, ActivationFunctionType
 
 CAP = 64
 PW = 384
-EARLY = 128
+FIRST = 2
+EARLY = [(1, (0, 16)), (3, (0, 12))]
 
 SCRATCH = {}
 
@@ -14,29 +15,30 @@ def _bufs(dtype, names):
         SCRATCH[name] = ("sbuf", [128, int(width)], dtype)
 
 
-_bufs("bfloat16", "xb:1280 usb:32 usr:512 zt:8192 n16:256 mk:256 rst:256")
+_bufs("bfloat16", "xb:1280 usb:32 usr:512 zt:8192 n16:128 mk:128 rst:128")
 _bufs("float8_e4m3fn_x4", "uq:128 xq:256 wq:3072 lc:448")
 _bufs("uint8", "up:128 xp:256 wp:3072 lp:448")
 _bufs("int32", "pidx:2 pci:6 uli:32 bci:8")
 _bufs("uint16", "ul:32 bc:8 gl:2 offu:16 cl:16 rn:16 lst:128")
-_bufs("float32", "pcf:3 n4:64 mk4:64 cap4:64 tc65:16 tc64:16 j4:256 c96:96 tab:384")
-_bufs("float32", "sm:256 sc:256 sl:96 ga:96 eo:16 xo:32 cop:40 exo:32 bto:32 n1:16 n2:16 zz:16 wd:2240 wm:64 ws:64")
+_bufs("float32", "pcf:6 n4:64 n32:32 mk4:64 cap4:64 above:32 tc65:16 tc64:16 j4:256 c96:96 tab:384")
+_bufs("float32", "sm:256 sc:256 sl:96 ga:96 eo:64 xo:48 cop:32 exo:32 n1:16 n2:16 zz:16 wd:2240 wm:64 ws:64")
 _bufs("float32", "m1:48 c1:48 xa:48 ya:48 aa:48 ee:96 cs:96 csb:96 ctp:104 ex:96 bt:96 kk:96 ke:96 t48:48 t16:16 x32:32 xt:32")
-_bufs("float32", "xg:32 xr:32 wv:256 acc:768")
+_bufs("float32", "xg:32 xr:32 wv:256 acc:768 side:768")
 _bufs("float32", "pw:%d" % (24 * PW))
 for _b in range(8):
     SCRATCH["ps%d" % _b] = ("psum", [128, 512], "float32")
 
-SEMAPHORES = ["sv", "ss", "st", "sg", "dx", "du", "ls", "dn", "dy"]
+SEMAPHORES = ["sv", "ss", "st", "sg", "dx0", "dx1", "du", "l0", "ls", "dn", "dy", "da", "dt0", "dt1", "dt2"]
 SEMAPHORES += ["%s%d" % (_n, _a) for _n in ("dw", "rs", "rc") for _a in range(6)]
 
 ADD, SUB, MUL, AND = AluOpType.add, AluOpType.subtract, AluOpType.mult, AluOpType.bitwise_and
 MIN, MAX, GT, GE, EQ = AluOpType.min, AluOpType.max, AluOpType.is_gt, AluOpType.is_ge, AluOpType.is_equal
+SHR = AluOpType.logical_shift_right
 COPY = ActivationFunctionType.Copy
 
-TILES = "000110101012020212121222"
-ITEMS = [(int(_o), TILES[:_n].count(_o)) for _n, _o in enumerate(TILES)]
-BY_SCALAR = [(1, 0), (2, 0)]
+TILES = "000110101010021212122222"
+BY_SCALAR = [(1, 0), (2, 0), (0, 4), (1, 3)]
+HALVES = 19
 
 
 def rank_program(g, core, T, topo):
@@ -79,6 +81,9 @@ def rank_program(g, core, T, topo):
     def ts(out, a, scalar, op):
         return v(V.tensor_scalar(out, a, scalar, None, op))
 
+    def ts2(out, a, s1, op0, s2, op1):
+        return v(V.tensor_scalar(out, a, s1, s2, op0, op1))
+
     def scan(out, a, b, op0, op1):
         return v(V.tensor_tensor_scan(out, a, b, 0.0, op0, op1))
 
@@ -94,24 +99,26 @@ def rank_program(g, core, T, topo):
         return done("sg", g.iota(out, pattern, base, cm))
 
     S.dma_start(T.usb[:, :], T.us[:, 0:32]).then_inc(T.sem.du, 16)
-    Y.dma_start(T.xb[:, 0:1024], T.x[:, :]).then_inc(T.sem.dx, 16)
+    for k in range(2):
+        Y.dma_start(T.xb[:, 512 * k:512 * k + 512], T.x[:, 512 * k:512 * k + 512]).then_inc(T.sem["dx%d" % k], 16)
 
     i_ul = iota(T.uli[:, :], [[1, 4], [4, 8]], 0, 0, False)
     i_p = iota(T.pidx[:, :], [[0, 2]], 0, 1, False)
-    i_n16 = iota(T.n16[:, :], [[0, 16], [1, 16]])
+    i_n16 = iota(T.n16[:, :], [[0, 8], [1, 16]])
     iota(T.n4[:, :], [[0, 16], [1, 4]])
+    iota(T.n32[:, :], [[1, 32]])
     i_bc = iota(T.bci[:, :], [[16, 8]], 15, 0, False)
 
     def zeros(b, e):
         return v(V.memset(T.zt[:, b:e], 0.0))
 
-    def zeros_s(b, e):
+    def zeros_s(b, e, z):
         for k in range(b, e, 512):
-            a = s_(S.activation(T.zt[:, k:k + 512], T.zt[:, 7680:8192], COPY))
+            a = s_(S.activation(T.zt[:, k:k + 512], T.zt[:, z:z + 512], COPY))
         return a
 
-    wait("s", "sv", zeros(7680, 8192))
-    s_z = [zeros_s(1024, 2048)]
+    wait("s", "sv", zeros(3584, 4096))
+    s_z = [zeros_s(1024, 2048, 3584)]
     wait("v", "sg", i_ul)
     c_ul = copy(T.ul[:, :], T.uli[:, :])
     wait("v", "sg", i_p)
@@ -129,14 +136,47 @@ def rank_program(g, core, T, topo):
     for t in range(2):
         c_u = copy(T.usr[:, t:512:4], T.usb[:, :].indirect(T.ul[:, 8 * t:8 * t + 8]))
         s_u = s_(S.activation(T.usr[:, t + 2:512:4], T.usb[:, :].indirect(T.ul[:, 8 * t + 16:8 * t + 24]), COPY))
-    s_z += [zeros_s(2048, 3072), zeros_s(4096, 6144), zeros_s(6144, 7680)]
-    zeros(3072, 3584)
+    s_z.append(zeros_s(2048, 3584, 3584))
+    wait("v", "dx0", 16)
+    v(V.quantize_mx(T.xq[:, 0:128], T.xp[:, 0:128], T.xb[:, 0:512]))
     vw(c_u)
     wait("v", "ss", s_u)
-    v(V.quantize_mx(T.uq[:, :], T.up[:, :], T.usr[:, :]))
-    wait("v", "dx", 16)
-    c_xq = v(V.quantize_mx(T.xq[:, :], T.xp[:, :], T.xb[:, 0:1024]))
-    c_z1 = zeros(3584, 4096)
+    c_xq = [v(V.quantize_mx(T.uq[:, :], T.up[:, :], T.usr[:, :]))]
+    wait("v", "dx1", 16)
+    c_xq.append(v(V.quantize_mx(T.xq[:, 128:256], T.xp[:, 128:256], T.xb[:, 512:1024])))
+
+    c_ps = []
+    vw(max(c_mk, c_rst))
+    for k in range(2):
+        bank, b, e = T["ps%d" % k], 128 * k, 128 * k + 128
+        wait("t", "sv", c_xq[k])
+        wait("v", "st", t_(TE.matmul_mx(bank[:, 0:128], T.uq[:, :], T.up[:, :], T.xq[:, b:e], T.xp[:, b:e], True, True)))
+        c_ps.append(tt(T.sm[:, b:e], bank[:, 0:128], T.mk[:, :], MUL))
+    for k in range(2):
+        vw(c_ps[k])
+        a = scan(T.sc[:, 128 * k:128 * k + 128], T.rst[:, :], T.sm[:, 128 * k:128 * k + 128], MUL, ADD)
+    vw(a)
+    e0 = order.index(r)
+    mine = T.sl[:, 16 * e0:16 * e0 + 16]
+    c_so = copy(mine, T.sc[:, 15:256:16])
+    wait("s", "sv", zeros(7680, 8192))
+    s_z += [zeros_s(4096, 6144, 7680), zeros_s(6144, 7680, 7680)]
+
+    turn = [(r + k) % N for k in range(1, N)]
+    dst_id, emask = {}, None
+    for s in turn:
+        rid, pid, _se = topo.addr(T.cores[s])
+        dst_id[s] = DstId(rid=rid, pnc=pid)
+        m = topo.mask(core, T.cores[s])
+        emask = m if emask is None else emask & m
+    ne = len([b for b in range(16) if emask >> b & 1])
+
+    def send(src, to, dsts, sem, left="ls"):
+        g.remote_dma_fused([RemoteDMATransfer(dst_ids=[dst_id[s] for s in to], dma_engine_mask=emask, remote_sem=T.sem[sem],
+                                              srcs=[src], dsts=dsts)], local_sem=T.sem[left])
+
+    wait("g", "sv", c_so)
+    send(mine, turn, [mine for _s in turn], "rs%d" % r, "l0")
 
     place = [0, 2048, 0, 2048, 4096, 6144]
 
@@ -157,69 +197,43 @@ def rank_program(g, core, T, topo):
             c_w[4 * c + k] = a
         return a
 
-    wait("y", "dx", 16)
+    wait("y", "dx1", 16)
     wait("y", "sv", c_z0)
     wait("y", "ss", s_z[0])
     load_w(0)
-    wait("y", "sv", c_z1)
     wait("y", "ss", s_z[1])
     load_w(1)
 
-    wait("t", "sv", c_xq)
-    p_s = t_(TE.matmul_mx(T.ps0[:, 0:256], T.uq[:, 0:128], T.up[:, 0:128], T.xq[:, 0:256], T.xp[:, 0:256], True, True))
-    wait("v", "st", p_s)
-    vw(c_mk)
-    c_ps0 = tt(T.sm[:, :], T.ps0[:, 0:256], T.mk[:, :], MUL)
-    vw(max(c_ps0, c_rst))
-    a = scan(T.sc[:, :], T.rst[:, :], T.sm[:, :], MUL, ADD)
-    vw(a)
-    e0 = order.index(r)
-    mine = T.sl[:, 16 * e0:16 * e0 + 16]
-    c_so = copy(mine, T.sc[:, 15:256:16])
-
-    turn = [(r + k) % N for k in range(1, N)]
-    dst_id, emask = {}, None
-    for s in turn:
-        rid, pid, _se = topo.addr(T.cores[s])
-        dst_id[s] = DstId(rid=rid, pnc=pid)
-        m = topo.mask(core, T.cores[s])
-        emask = m if emask is None else emask & m
-    ne = len([b for b in range(16) if emask >> b & 1])
-
-    def send(src, to, dsts, sem):
-        g.remote_dma_fused([RemoteDMATransfer(dst_ids=[dst_id[s] for s in to], dma_engine_mask=emask, remote_sem=T.sem[sem],
-                                              srcs=[src], dsts=dsts)], local_sem=T.sem.ls)
-
-    wait("g", "sv", c_so)
-    send(mine, turn, [mine for _s in turn], "rs%d" % r)
-
-    iota(T.xo[:, 16:32], [[0, 16]])
-    iota(T.cop[:, 0:1], [[0, 1]])
-    iota(T.tc65[:, :], [[1, 16]], CAP + 1, 16)
-    i_z1 = iota(T.tc64[:, :], [[1, 16]], CAP, 16)
+    iota(T.eo[:, 16:64], [[0, 48]])
+    iota(T.tc65[:, :], [[1, 16]], CAP + 1 + 16 * 127, -16)
+    i_z1 = iota(T.tc64[:, :], [[1, 16]], CAP + 16 * 127, -16)
     iota(T.wd[:, 0:64], [[0, 64]])
     iota(T.cap4[:, :], [[0, 16], [2048, 4]])
     i_j4 = iota(T.j4[:, :], [[4, 256]])
-    iota(T.ctp[:, 0:1], [[0, 1]])
+    iota(T.ctp[:, 96:97], [[0, 1]])
     for e, s in enumerate(order):
         i_c = iota(T.c96[:, 16 * e:16 * e + 16], [[0, 16]], CAP * ((r - s) % N) - 1)
     i_tab = iota(T.tab[:, 0:CAP * (r + 1)], [[-1, r + 1], [0, CAP]], r)
     if r + 1 < N:
         i_tab = iota(T.tab[:, CAP * (r + 1):PW], [[-1, N - r - 1], [0, CAP]], N - 1)
 
-    wait("y", "sv", quant_w(0))
-    load_w(2)
     wait("v", "sg", i_bc)
     ts(T.pci[:, 1:2], T.pidx[:, 0:1], 3, AND)
-    v(V.tensor_scalar(T.pci[:, 2:3], T.pidx[:, 0:1], 2, 3, AluOpType.logical_shift_right, AND))
+    ts2(T.pci[:, 2:3], T.pidx[:, 0:1], 2, SHR, 3, AND)
+    ts2(T.pci[:, 3:4], T.pidx[:, 0:1], 4, SHR, 1, AND)
     a = ts(T.pci[:, 4:6], T.pidx[:, 0:2], 31, AND)
+    quant_w(0)
+    vw(a)
+    a = copy(T.pcf[:, 1:6], T.pci[:, 1:6])
+    copy(T.gl[:, :], T.pci[:, 4:6])
     copy(T.bc[:, :], T.bci[:, :])
     vw(a)
-    a = copy(T.pcf[:, 1:3], T.pci[:, 1:3])
-    copy(T.gl[:, :], T.pci[:, 4:6])
-    vw(a)
+    ts(T.above[:, 0:16], T.n32[:, 0:16], T.pcf[:, 4:5], GT)
+    ts2(T.above[:, 16:32], T.n32[:, 16:32], T.pcf[:, 4:5], GT, T.pcf[:, 3:4], MUL)
     c_cst = ts(T.mk4[:, :], T.n4[:, :], T.pcf[:, 2:3], EQ)
     wait("y", "sv", quant_w(1))
+    wait("y", "l0", ne)
+    load_w(2)
     load_w(3)
     wait("y", "ss", s_z[2])
     load_w(4)
@@ -241,9 +255,9 @@ def rank_program(g, core, T, topo):
         ("e1", ["aa"], lambda: tt(T.ee[:, 48:96], T.aa[:, :], T.c1[:, :], MUL)),
         ("e0", ["aa"], lambda: tt(T.ee[:, 0:48], T.aa[:, :], T.c1[:, :], GT)),
         ("cs", ["e0"], lambda: scan(T.cs[:, :], T.rst[:, 0:96], T.ee[:, :], MUL, ADD)),
-        ("ct", ["cs"], lambda: need("sg", i_c, lambda: turn32(T.ctp[:, 1:97], T.cs[:, :]))),
+        ("ct", ["cs"], lambda: need("sg", i_c, lambda: turn32(T.ctp[:, 0:96], T.cs[:, :]))),
         ("cb", ["cs"], lambda: tt(T.csb[:, :], T.cs[:, :], T.c96[:, :], ADD)),
-        ("ex", ["ct"], lambda: scan(T.ex[:, :], T.ctp[:, 0:96], T.rst[:, 0:96], ADD, MUL)),
+        ("ex", ["ct"], lambda: scan(T.ex[:, ::-1], T.ctp[:, 96:0:-1], T.rst[:, 0:96], ADD, MUL)),
         ("bt", ["ex"], lambda: turn32(T.bt[:, :], T.ex[:, :])),
         ("kk", ["bt"], lambda: tt(T.kk[:, :], T.bt[:, :].indirect(T.bc[:, 0:6]), T.csb[:, :], ADD)),
         ("ke", ["kk"], lambda: tt(T.ke[:, :], T.kk[:, :], T.ee[:, :], MUL)),
@@ -270,35 +284,34 @@ def rank_program(g, core, T, topo):
 
     vw(c_cst)
     c_eo = None
+    eo = T.eo[:, 0:16]
     for s in reversed(turn):
         wait("v", "rs%d" % s, ne)
         e = order.index(s)
         op = GT if s < r else GE
         if c_eo is None:
-            c_eo = tt(T.eo[:, :], mine, T.sl[:, 16 * e:16 * e + 16], op)
+            c_eo = tt(eo, mine, T.sl[:, 16 * e:16 * e + 16], op)
         else:
             k = 16 * turn.index(s)
             a = tt(T.ga[:, k:k + 16], mine, T.sl[:, 16 * e:16 * e + 16], op)
             if s == turn[0]:
                 fill()
             vw(a)
-            c_eo = tt(T.eo[:, :], T.eo[:, :], T.ga[:, k:k + 16], MUL)
+            c_eo = tt(eo, eo, T.ga[:, k:k + 16], MUL)
     wait("v", "sg", i_z1)
     after(c_eo)
-    c_co = scan(T.xo[:, 0:16], T.rst[:, 0:16], T.eo[:, :], MUL, ADD)
-    c_n1 = tt(T.n1[:, :], T.eo[:, :], T.tc65[:, :], MUL)
+    c_co = scan(T.xo[:, :], T.eo[:, 16:64], T.eo[:, 0:48], ADD, ADD)
+    c_n1 = tt(T.n1[:, :], eo, T.tc65[:, :], MUL)
     vw(c_co)
-    a = turn32(T.cop[:, 1:33], T.xo[:, :])
+    a = turn32(T.cop[:, :], T.xo[:, 16:48])
     vw(c_n1)
     c_n2 = tt(T.n2[:, :], T.tc64[:, :], T.n1[:, :], SUB)
     vw(a)
-    a = scan(T.exo[:, :], T.cop[:, 0:32], T.rst[:, 0:32], ADD, MUL)
+    a = scan(T.exo[:, :], T.cop[:, :], T.above[:, :], ADD, MUL)
     vw(c_n2)
     b = tt(T.zz[:, :], T.xo[:, 0:16], T.n2[:, :], ADD)
-    vw(a)
-    a = turn32(T.bto[:, :], T.exo[:, :])
     after(max(a, b))
-    a = ts(T.offu[:, :], T.zz[:, :], T.bto[:, 15:16], ADD)
+    a = ts2(T.offu[:, :], T.zz[:, :], T.exo[:, 15:16], ADD, T.exo[:, 31:32], ADD)
     wait("v", "sg", i_j4)
     after(a)
     a = copy(T.wd[:, :].indirect(T.offu[:, 0:16]), T.j4[:, :])
@@ -308,8 +321,9 @@ def rank_program(g, core, T, topo):
     a = scan(T.ws[:, :], T.cap4[:, :], T.wm[:, :], MIN, ADD)
     after(a)
     c_cl = ts(T.cl[:, :], T.ws[:, 3:64:4], T.pcf[:, 1:2], ADD)
+    wait("s", "dx0", 16)
+    wait("s", "dx1", 16)
     wait("s", "sv", c_cl)
-    wait("s", "dx", 16)
     s_h = s_(S.activation(T.xb[:, 1152:1280], T.xb[:, 0:1024].indirect(T.cl[:, 8:16]), COPY))
     after(c_cl)
     a = copy(T.xb[:, 1024:1152], T.xb[:, 0:1024].indirect(T.cl[:, 0:8]))
@@ -321,68 +335,94 @@ def rank_program(g, core, T, topo):
         return [buf[:, CAP * (2 + turn.index(s)):CAP * (3 + turn.index(s))] for s in to]
 
     wait("g", "sv", c_hq)
-    send(T.lp[:, CAP:2 * CAP], turn[:1], lands(T.lp, turn[:1]), "rc%d" % r)
+    send(T.lp[:, CAP:2 * CAP], turn[:FIRST], lands(T.lp, turn[:FIRST]), "rc%d" % r)
     send(T.lc[:, CAP:2 * CAP].bitcast(dt.uint8), turn, [x.bitcast(dt.uint8) for x in lands(T.lc, turn)], "rc%d" % r)
-    send(T.lp[:, CAP:2 * CAP], turn[1:], lands(T.lp, turn[1:]), "rc%d" % r)
+    send(T.lp[:, CAP:2 * CAP], turn[FIRST:], lands(T.lp, turn[FIRST:]), "rc%d" % r)
 
-    tiles = [(c, f) for c in (2, 3) for f in range(4)]
+    tiles = [(c, f) for c in range(2, 6) for f in range(4)]
     while len(at) < len(steps):
-        if tiles and count["sv"] in [at[x] for x in steps[len(at)][1]]:
+        if count["sv"] in [at[x] for x in steps[len(at)][1]]:
             quant_w(*tiles.pop(0), 1)
         fill()
     vw(at["xr"])
     for k in range(4):
         a = copy(T.lst[0:32, 32 * k:32 * k + 32], T.xr[32 * k:32 * k + 32, :])
-    quant_w(4)
+    quant_w(*tiles.pop(0), 1)
     vw(a)
     for k in range(1, 4):
         c_lst = copy(T.lst[32 * k:32 * k + 32, :], T.lst[0:32, :])
-    quant_w(5)
+    for c, f in tiles:
+        quant_w(c, f, 1)
+    wait("v", "sg", i_tab)
+    wait("y", "sv", copy(T.wv[:, :], T.tab[:, :].indirect(T.rn[:, :])))
+    for h in range(8):
+        Y.dma_start(T.wn[h:h + 1, :], T.wv[16 * h:16 * h + 1, :]).then_inc(T.sem.dn, 16)
 
-    bank_free = [("sv", c_ps0)] + [None] * 7
+    bank_free = [("sv", c_ps[0]), ("sv", c_ps[1])] + [None] * 6
     made = [0]
+    have = {}
 
-    def product(o, h, b, e):
+    def product(o, h, e):
         n = made[0] % 8
         made[0] += 1
         bank, w = T["ps%d" % n], 1024 * o + 128 * h
+        b = have.get((o, h), 0)
+        have[(o, h)] = e
+        m = min(b, e - 128)
         wait("t", "sv", c_w[8 * o + h])
         if bank_free[n] is not None:
             wait("t", *bank_free[n])
-        p = t_(TE.matmul_mx(bank[:, 0:e - b], T.wq[:, w:w + 128], T.wp[:, w:w + 128],
-                            T.lc[:, CAP + b:CAP + e], T.lp[:, CAP + b:CAP + e], True, True))
+        p = t_(TE.matmul_mx(bank[:, 0:e - m], T.wq[:, w:w + 128], T.wp[:, w:w + 128],
+                            T.lc[:, CAP + m:CAP + e], T.lp[:, CAP + m:CAP + e], True, True))
         wait("s", "st", p)
         w0 = PW * (8 * o + h)
-        bank_free[n] = ("ss", s_(S.activation(T.pw[:, w0 + b:w0 + e], bank[:, 0:e - b], COPY)))
+        bank_free[n] = ("ss", s_(S.activation(T.pw[:, w0 + b:w0 + e], bank[:, b - m:e - m], COPY)))
         return bank_free[n][1]
 
     wait("t", "sv", c_hq)
-    wait("t", "rc%d" % turn[-1], 2 * ne)
-    for o in range(2):
-        if o == 1:
-            wait("s", "sv", at["rn"])
-            wait("s", "sg", i_tab)
-            wait("y", "ss", s_(S.activation(T.wv[:, :], T.tab[:, :].indirect(T.rn[:, :]), COPY)))
-            for h in range(8):
-                Y.dma_start(T.wn[h:h + 1, :], T.wv[16 * h:16 * h + 1, :]).then_inc(T.sem.dn, 16)
-        for h in range(8):
-            product(o, h, 0, EARLY)
-    for s in turn[:-1]:
+    for blocks, n in EARLY:
+        for s in turn[N - blocks:]:
+            wait("t", "rc%d" % s, 2 * ne)
+        for k in range(*n):
+            product(k // 8, k % 8, CAP * blocks)
+    for s in turn:
         wait("t", "rc%d" % s, 2 * ne)
 
-    last = {}
-    for n, (o, h) in enumerate(ITEMS):
-        c = product(o, h, EARLY if o < 2 else 0, PW)
+    items = [(int(o), TILES[:n].count(o)) for n, o in enumerate(TILES)]
+    last, aside, pending, stores = {}, [], [], {"da": 0, "dy": 0}
+
+    def add_to_y(o, src, ready):
+        wait("g", *ready)
+        wait("g", "dt%d" % o, 16)
+        g.dma_start(T.y[:, 256 * o:256 * o + 256], src, accum_op=ADD).then_inc(T.sem.da, 16)
+        stores["da"] += 16
+
+    def by_scalar():
+        o, h, c = pending.pop()
         win = T.pw[:, PW * (8 * o + h):PW * (8 * o + h + 1)]
+        wait("s", "ss", c)
+        wait("s", "sv", c_lst)
+        out = T.side[:, 256 * len(aside):256 * len(aside) + 256] if h else T.acc[:, 256 * o:256 * o + 256]
+        a = ("ss", s_(S.activation(out, win.indirect(T.lst[:, 16 * h:16 * h + 16]), COPY)))
+        if h == 0:
+            last[o] = [a, a]
+        else:
+            wait("y", *a)
+            Y.dma_start(T.y[:, 256 * o:256 * o + 256], out).then_inc(T.sem["dt%d" % o], 16)
+            aside.append(o)
+
+    for n, (o, h) in enumerate(items):
+        c = product(o, h, PW)
+        if pending:
+            by_scalar()
         if (o, h) in BY_SCALAR:
-            wait("s", "ss", c)
-            wait("s", "sv", c_lst)
-            a = s_(S.activation(T.acc[:, 256 * o:256 * o + 256], win.indirect(T.lst[:, 16 * h:16 * h + 16]), COPY))
-            last[o] = [("ss", a), ("ss", a)]
+            pending.append((o, h, c))
             continue
+        win = T.pw[:, PW * (8 * o + h):PW * (8 * o + h + 1)]
         wait("v", "ss", c)
         vw(c_lst)
-        m = 8 if n >= 22 else 16
+        final = all(x in BY_SCALAR or x[0] != o for x in items[n + 1:])
+        m = 8 if n >= HALVES else 16
         for f in range(16 // m):
             acc = T.acc[:, 256 * o + 128 * f:256 * o + 128 * f + 16 * m]
             picked = win.indirect(T.lst[:, 16 * h + 8 * f:16 * h + 8 * f + m])
@@ -392,12 +432,16 @@ def rank_program(g, core, T, topo):
             else:
                 a = ("sv", copy(acc, picked))
             last[o] = [a, a] if m == 16 else ([a, last[o][1]] if f == 0 else [last[o][0], a])
-            if h == 7:
+            if final and o in aside:
+                add_to_y(o, acc, a)
+            elif final:
                 wait("y", *a)
                 Y.dma_start(T.y[:, 256 * o + 128 * f:256 * o + 128 * f + 16 * m], acc).then_inc(T.sem.dy, 16)
+                stores["dy"] += 16
 
-    wait("y", "dy", 64)
+    wait("y", "dy", stores["dy"])
     wait("y", "dn", 128)
-    wait("g", "ls", 4 * ne)
+    wait("g", "da", stores["da"])
+    wait("g", "ls", 3 * ne)
     for sem in ("sv", "ss", "st", "sg"):
         wait("g", sem, count[sem])

from concourse.bass import DstId, RemoteDMATransfer
from concourse.mybir import dt, AluOpType, ActivationFunctionType

CAP = 64
PW = 384
FIRST = 2
EARLY = [(1, (0, 16)), (3, (0, 12))]

SCRATCH = {}


def _bufs(dtype, names):
    for item in names.split():
        name, width = item.split(":")
        SCRATCH[name] = ("sbuf", [128, int(width)], dtype)


_bufs("bfloat16", "xb:1280 usb:32 usr:512 zt:8192 n16:128 mk:128 rst:128")
_bufs("float8_e4m3fn_x4", "uq:128 xq:256 wq:3072 lc:448")
_bufs("uint8", "up:128 xp:256 wp:3072 lp:448")
_bufs("int32", "pidx:2 pci:6 uli:32 bci:8")
_bufs("uint16", "ul:32 bc:8 gl:2 offu:16 cl:16 rn:16 lst:128")
_bufs("float32", "pcf:6 n4:64 n32:32 mk4:64 cap4:64 above:32 tc65:16 tc64:16 j4:256 c96:96 tab:384")
_bufs("float32", "sm:256 sc:256 sl:96 ga:96 eo:64 xo:48 cop:32 exo:32 n1:16 n2:16 zz:16 wd:2240 wm:64 ws:64")
_bufs("float32", "m1:48 c1:48 xa:48 ya:48 aa:48 ee:96 cs:96 csb:96 ctp:104 ex:96 bt:96 kk:96 ke:96 t48:48 t16:16 x32:32 xt:32")
_bufs("float32", "xg:32 xr:32 wv:256 acc:768 side:768")
_bufs("float32", "pw:%d" % (24 * PW))
for _b in range(8):
    SCRATCH["ps%d" % _b] = ("psum", [128, 512], "float32")

SEMAPHORES = ["sv", "ss", "st", "sg", "dx0", "dx1", "du", "l0", "ls", "dn", "dy", "da", "dt0", "dt1", "dt2"]
SEMAPHORES += ["%s%d" % (_n, _a) for _n in ("dw", "rs", "rc") for _a in range(6)]

ADD, SUB, MUL, AND = AluOpType.add, AluOpType.subtract, AluOpType.mult, AluOpType.bitwise_and
MIN, MAX, GT, GE, EQ = AluOpType.min, AluOpType.max, AluOpType.is_gt, AluOpType.is_ge, AluOpType.is_equal
SHR = AluOpType.logical_shift_right
COPY = ActivationFunctionType.Copy

TILES = "000110101010021212122222"
BY_SCALAR = [(1, 0), (2, 0), (0, 4), (1, 3)]
HALVES = 19


def rank_program(g, core, T, topo):
    r = T.rank_of(core)
    if r is None:
        return
    N = len(T.cores)
    order = [s for s in range(N) if s % 2 == 0] + [s for s in range(N) if s % 2 == 1]

    queues = {"g": g, "v": g.vector, "s": g.scalar, "t": g.tensor, "y": g.sync}
    V, S, TE, Y = g.vector, g.scalar, g.tensor, g.sync
    count = {"sv": 0, "ss": 0, "st": 0, "sg": 0}
    seen = {}

    def wait(q, sem, n):
        if n > seen.get((q, sem), 0):
            queues[q].wait_ge(T.sem[sem], n)
            seen[(q, sem)] = n

    def done(sem, ins):
        ins.then_inc(T.sem[sem], 1)
        count[sem] += 1
        return count[sem]

    def v(ins):
        return done("sv", ins)

    def s_(ins):
        return done("ss", ins)

    def t_(ins):
        return done("st", ins)

    def vw(n):
        wait("v", "sv", n)

    def tt(out, a, b, op):
        return v(V.tensor_tensor(out, a, b, op))

    def ts(out, a, scalar, op):
        return v(V.tensor_scalar(out, a, scalar, None, op))

    def ts2(out, a, s1, op0, s2, op1):
        return v(V.tensor_scalar(out, a, s1, s2, op0, op1))

    def scan(out, a, b, op0, op1):
        return v(V.tensor_tensor_scan(out, a, b, 0.0, op0, op1))

    def copy(out, a):
        return v(V.tensor_copy(out, a))

    def turn32(out, a):
        return v(V.transpose(out, a))

    def iota(out, pattern, base=0, cm=0, flag=True):
        if flag:
            return done("sg", g.iota(out, pattern, base, cm, allow_small_or_imprecise_dtypes=True))
        return done("sg", g.iota(out, pattern, base, cm))

    S.dma_start(T.usb[:, :], T.us[:, 0:32]).then_inc(T.sem.du, 16)
    for k in range(2):
        Y.dma_start(T.xb[:, 512 * k:512 * k + 512], T.x[:, 512 * k:512 * k + 512]).then_inc(T.sem["dx%d" % k], 16)

    i_ul = iota(T.uli[:, :], [[1, 4], [4, 8]], 0, 0, False)
    i_p = iota(T.pidx[:, :], [[0, 2]], 0, 1, False)
    i_n16 = iota(T.n16[:, :], [[0, 8], [1, 16]])
    iota(T.n4[:, :], [[0, 16], [1, 4]])
    iota(T.n32[:, :], [[1, 32]])
    i_bc = iota(T.bci[:, :], [[16, 8]], 15, 0, False)

    def zeros(b, e):
        return v(V.memset(T.zt[:, b:e], 0.0))

    def zeros_s(b, e, z):
        for k in range(b, e, 512):
            a = s_(S.activation(T.zt[:, k:k + 512], T.zt[:, z:z + 512], COPY))
        return a

    wait("s", "sv", zeros(3584, 4096))
    s_z = [zeros_s(1024, 2048, 3584)]
    wait("v", "sg", i_ul)
    c_ul = copy(T.ul[:, :], T.uli[:, :])
    wait("v", "sg", i_p)
    a = ts(T.pci[:, 0:1], T.pidx[:, 0:1], 15, AND)
    c_z0 = zeros(0, 1024)
    vw(a)
    a = copy(T.pcf[:, 0:1], T.pci[:, 0:1])
    wait("v", "sg", i_n16)
    c_rst = ts(T.rst[:, :], T.n16[:, :], 0.0, GT)
    vw(a)
    c_mk = ts(T.mk[:, :], T.n16[:, :], T.pcf[:, 0:1], EQ)
    wait("v", "du", 16)
    wait("s", "du", 16)
    wait("s", "sv", c_ul)
    for t in range(2):
        c_u = copy(T.usr[:, t:512:4], T.usb[:, :].indirect(T.ul[:, 8 * t:8 * t + 8]))
        s_u = s_(S.activation(T.usr[:, t + 2:512:4], T.usb[:, :].indirect(T.ul[:, 8 * t + 16:8 * t + 24]), COPY))
    s_z.append(zeros_s(2048, 3584, 3584))
    wait("v", "dx0", 16)
    v(V.quantize_mx(T.xq[:, 0:128], T.xp[:, 0:128], T.xb[:, 0:512]))
    vw(c_u)
    wait("v", "ss", s_u)
    c_xq = [v(V.quantize_mx(T.uq[:, :], T.up[:, :], T.usr[:, :]))]
    wait("v", "dx1", 16)
    c_xq.append(v(V.quantize_mx(T.xq[:, 128:256], T.xp[:, 128:256], T.xb[:, 512:1024])))

    c_ps = []
    vw(max(c_mk, c_rst))
    for k in range(2):
        bank, b, e = T["ps%d" % k], 128 * k, 128 * k + 128
        wait("t", "sv", c_xq[k])
        wait("v", "st", t_(TE.matmul_mx(bank[:, 0:128], T.uq[:, :], T.up[:, :], T.xq[:, b:e], T.xp[:, b:e], True, True)))
        c_ps.append(tt(T.sm[:, b:e], bank[:, 0:128], T.mk[:, :], MUL))
    for k in range(2):
        vw(c_ps[k])
        a = scan(T.sc[:, 128 * k:128 * k + 128], T.rst[:, :], T.sm[:, 128 * k:128 * k + 128], MUL, ADD)
    vw(a)
    e0 = order.index(r)
    mine = T.sl[:, 16 * e0:16 * e0 + 16]
    c_so = copy(mine, T.sc[:, 15:256:16])
    wait("s", "sv", zeros(7680, 8192))
    s_z += [zeros_s(4096, 6144, 7680), zeros_s(6144, 7680, 7680)]

    turn = [(r + k) % N for k in range(1, N)]
    dst_id, emask = {}, None
    for s in turn:
        rid, pid, _se = topo.addr(T.cores[s])
        dst_id[s] = DstId(rid=rid, pnc=pid)
        m = topo.mask(core, T.cores[s])
        emask = m if emask is None else emask & m
    ne = len([b for b in range(16) if emask >> b & 1])

    def send(src, to, dsts, sem, left="ls"):
        g.remote_dma_fused([RemoteDMATransfer(dst_ids=[dst_id[s] for s in to], dma_engine_mask=emask, remote_sem=T.sem[sem],
                                              srcs=[src], dsts=dsts)], local_sem=T.sem[left])

    wait("g", "sv", c_so)
    send(mine, turn, [mine for _s in turn], "rs%d" % r, "l0")

    place = [0, 2048, 0, 2048, 4096, 6144]

    def load_w(c):
        o, f = c // 2, 4 * (c % 2)
        for h in range(f, f + 4):
            z = place[c] + 512 * (h - f)
            Y.dma_start(T.zt[16 * h:16 * h + 16, z:z + 512],
                        T.w[16 * h:16 * h + 16, 512 * o:512 * o + 512]).then_inc(T.sem["dw%d" % c], 16)

    c_w = {}

    def quant_w(c, f=0, n=4):
        wait("v", "dw%d" % c, 64)
        b, e = 512 * c + 128 * f, 512 * c + 128 * (f + n)
        a = v(V.quantize_mx(T.wq[:, b:e], T.wp[:, b:e], T.zt[:, place[c] + 512 * f:place[c] + 512 * (f + n)]))
        for k in range(f, f + n):
            c_w[4 * c + k] = a
        return a

    wait("y", "dx1", 16)
    wait("y", "sv", c_z0)
    wait("y", "ss", s_z[0])
    load_w(0)
    wait("y", "ss", s_z[1])
    load_w(1)

    iota(T.eo[:, 16:64], [[0, 48]])
    iota(T.tc65[:, :], [[1, 16]], CAP + 1 + 16 * 127, -16)
    i_z1 = iota(T.tc64[:, :], [[1, 16]], CAP + 16 * 127, -16)
    iota(T.wd[:, 0:64], [[0, 64]])
    iota(T.cap4[:, :], [[0, 16], [2048, 4]])
    i_j4 = iota(T.j4[:, :], [[4, 256]])
    iota(T.ctp[:, 96:97], [[0, 1]])
    for e, s in enumerate(order):
        i_c = iota(T.c96[:, 16 * e:16 * e + 16], [[0, 16]], CAP * ((r - s) % N) - 1)
    i_tab = iota(T.tab[:, 0:CAP * (r + 1)], [[-1, r + 1], [0, CAP]], r)
    if r + 1 < N:
        i_tab = iota(T.tab[:, CAP * (r + 1):PW], [[-1, N - r - 1], [0, CAP]], N - 1)

    wait("v", "sg", i_bc)
    ts(T.pci[:, 1:2], T.pidx[:, 0:1], 3, AND)
    ts2(T.pci[:, 2:3], T.pidx[:, 0:1], 2, SHR, 3, AND)
    ts2(T.pci[:, 3:4], T.pidx[:, 0:1], 4, SHR, 1, AND)
    a = ts(T.pci[:, 4:6], T.pidx[:, 0:2], 31, AND)
    quant_w(0)
    vw(a)
    a = copy(T.pcf[:, 1:6], T.pci[:, 1:6])
    copy(T.gl[:, :], T.pci[:, 4:6])
    copy(T.bc[:, :], T.bci[:, :])
    vw(a)
    ts(T.above[:, 0:16], T.n32[:, 0:16], T.pcf[:, 4:5], GT)
    ts2(T.above[:, 16:32], T.n32[:, 16:32], T.pcf[:, 4:5], GT, T.pcf[:, 3:4], MUL)
    c_cst = ts(T.mk4[:, :], T.n4[:, :], T.pcf[:, 2:3], EQ)
    wait("y", "sv", quant_w(1))
    wait("y", "l0", ne)
    load_w(2)
    load_w(3)
    wait("y", "ss", s_z[2])
    load_w(4)
    wait("y", "ss", s_z[3])
    load_w(5)

    def need(sem, n, call):
        wait("v", sem, n)
        return call()

    steps = [
        ("m1", [], lambda: tt(T.m1[:, :], T.sl[:, 0:48], T.sl[:, 48:96], MAX)),
        ("c1", [], lambda: tt(T.c1[:, :], T.sl[:, 48:96], T.sl[:, 0:48], GT)),
        ("x0", ["m1"], lambda: tt(T.xa[:, 0:32], T.m1[:, 0:32], T.m1[:, 16:48], GE)),
        ("y1", ["m1"], lambda: tt(T.ya[:, 16:48], T.m1[:, 16:48], T.m1[:, 0:32], GT)),
        ("x1", ["m1"], lambda: tt(T.xa[:, 32:48], T.m1[:, 32:48], T.m1[:, 0:16], GT)),
        ("y0", ["m1"], lambda: tt(T.ya[:, 0:16], T.m1[:, 0:16], T.m1[:, 32:48], GE)),
        ("aa", ["y0"], lambda: tt(T.aa[:, :], T.xa[:, :], T.ya[:, :], MUL)),
        ("e1", ["aa"], lambda: tt(T.ee[:, 48:96], T.aa[:, :], T.c1[:, :], MUL)),
        ("e0", ["aa"], lambda: tt(T.ee[:, 0:48], T.aa[:, :], T.c1[:, :], GT)),
        ("cs", ["e0"], lambda: scan(T.cs[:, :], T.rst[:, 0:96], T.ee[:, :], MUL, ADD)),
        ("ct", ["cs"], lambda: need("sg", i_c, lambda: turn32(T.ctp[:, 0:96], T.cs[:, :]))),
        ("cb", ["cs"], lambda: tt(T.csb[:, :], T.cs[:, :], T.c96[:, :], ADD)),
        ("ex", ["ct"], lambda: scan(T.ex[:, ::-1], T.ctp[:, 96:0:-1], T.rst[:, 0:96], ADD, MUL)),
        ("bt", ["ex"], lambda: turn32(T.bt[:, :], T.ex[:, :])),
        ("kk", ["bt"], lambda: tt(T.kk[:, :], T.bt[:, :].indirect(T.bc[:, 0:6]), T.csb[:, :], ADD)),
        ("ke", ["kk"], lambda: tt(T.ke[:, :], T.kk[:, :], T.ee[:, :], MUL)),
        ("t3", ["ke"], lambda: tt(T.t48[:, :], T.ke[:, 0:48], T.ke[:, 48:96], ADD)),
        ("t2", ["t3"], lambda: tt(T.t16[:, :], T.t48[:, 0:16], T.t48[:, 16:32], ADD)),
        ("r0", ["t2"], lambda: tt(T.x32[:, 0:16], T.t16[:, :], T.t48[:, 32:48], ADD)),
        ("r1", ["t2"], lambda: tt(T.x32[:, 16:32], T.t16[:, :], T.t48[:, 32:48], ADD)),
        ("xt", ["r1"], lambda: turn32(T.xt[:, :], T.x32[:, :])),
        ("rn", ["r0"], lambda: copy(T.rn[:, :], T.x32[:, 0:16])),
        ("xg", ["xt"], lambda: copy(T.xg[:, :], T.xt[:, :].indirect(T.gl[:, :]))),
        ("xr", ["xg"], lambda: turn32(T.xr[:, :], T.xg[:, :])),
    ]
    at = {}

    def fill():
        name, reads, call = steps[len(at)]
        for x in reads:
            vw(at[x])
        at[name] = call()

    def after(n):
        fill()
        vw(n)

    vw(c_cst)
    c_eo = None
    eo = T.eo[:, 0:16]
    for s in reversed(turn):
        wait("v", "rs%d" % s, ne)
        e = order.index(s)
        op = GT if s < r else GE
        if c_eo is None:
            c_eo = tt(eo, mine, T.sl[:, 16 * e:16 * e + 16], op)
        else:
            k = 16 * turn.index(s)
            a = tt(T.ga[:, k:k + 16], mine, T.sl[:, 16 * e:16 * e + 16], op)
            if s == turn[0]:
                fill()
            vw(a)
            c_eo = tt(eo, eo, T.ga[:, k:k + 16], MUL)
    wait("v", "sg", i_z1)
    after(c_eo)
    c_co = scan(T.xo[:, :], T.eo[:, 16:64], T.eo[:, 0:48], ADD, ADD)
    c_n1 = tt(T.n1[:, :], eo, T.tc65[:, :], MUL)
    vw(c_co)
    a = turn32(T.cop[:, :], T.xo[:, 16:48])
    vw(c_n1)
    c_n2 = tt(T.n2[:, :], T.tc64[:, :], T.n1[:, :], SUB)
    vw(a)
    a = scan(T.exo[:, :], T.cop[:, :], T.above[:, :], ADD, MUL)
    vw(c_n2)
    b = tt(T.zz[:, :], T.xo[:, 0:16], T.n2[:, :], ADD)
    after(max(a, b))
    a = ts2(T.offu[:, :], T.zz[:, :], T.exo[:, 15:16], ADD, T.exo[:, 31:32], ADD)
    wait("v", "sg", i_j4)
    after(a)
    a = copy(T.wd[:, :].indirect(T.offu[:, 0:16]), T.j4[:, :])
    after(a)
    a = tt(T.wm[:, :], T.wd[:, 0:64], T.mk4[:, :], MUL)
    after(a)
    a = scan(T.ws[:, :], T.cap4[:, :], T.wm[:, :], MIN, ADD)
    after(a)
    c_cl = ts(T.cl[:, :], T.ws[:, 3:64:4], T.pcf[:, 1:2], ADD)
    wait("s", "dx0", 16)
    wait("s", "dx1", 16)
    wait("s", "sv", c_cl)
    s_h = s_(S.activation(T.xb[:, 1152:1280], T.xb[:, 0:1024].indirect(T.cl[:, 8:16]), COPY))
    after(c_cl)
    a = copy(T.xb[:, 1024:1152], T.xb[:, 0:1024].indirect(T.cl[:, 0:8]))
    after(a)
    wait("v", "ss", s_h)
    c_hq = v(V.quantize_mx(T.lc[:, 0:128], T.lp[:, 0:128], T.xb[:, 768:1280]))

    def lands(buf, to):
        return [buf[:, CAP * (2 + turn.index(s)):CAP * (3 + turn.index(s))] for s in to]

    wait("g", "sv", c_hq)
    send(T.lp[:, CAP:2 * CAP], turn[:FIRST], lands(T.lp, turn[:FIRST]), "rc%d" % r)
    send(T.lc[:, CAP:2 * CAP].bitcast(dt.uint8), turn, [x.bitcast(dt.uint8) for x in lands(T.lc, turn)], "rc%d" % r)
    send(T.lp[:, CAP:2 * CAP], turn[FIRST:], lands(T.lp, turn[FIRST:]), "rc%d" % r)

    tiles = [(c, f) for c in range(2, 6) for f in range(4)]
    while len(at) < len(steps):
        if count["sv"] in [at[x] for x in steps[len(at)][1]]:
            quant_w(*tiles.pop(0), 1)
        fill()
    vw(at["xr"])
    for k in range(4):
        a = copy(T.lst[0:32, 32 * k:32 * k + 32], T.xr[32 * k:32 * k + 32, :])
    quant_w(*tiles.pop(0), 1)
    vw(a)
    for k in range(1, 4):
        c_lst = copy(T.lst[32 * k:32 * k + 32, :], T.lst[0:32, :])
    for c, f in tiles:
        quant_w(c, f, 1)
    wait("v", "sg", i_tab)
    wait("y", "sv", copy(T.wv[:, :], T.tab[:, :].indirect(T.rn[:, :])))
    for h in range(8):
        Y.dma_start(T.wn[h:h + 1, :], T.wv[16 * h:16 * h + 1, :]).then_inc(T.sem.dn, 16)

    bank_free = [("sv", c_ps[0]), ("sv", c_ps[1])] + [None] * 6
    made = [0]
    have = {}

    def product(o, h, e):
        n = made[0] % 8
        made[0] += 1
        bank, w = T["ps%d" % n], 1024 * o + 128 * h
        b = have.get((o, h), 0)
        have[(o, h)] = e
        m = min(b, e - 128)
        wait("t", "sv", c_w[8 * o + h])
        if bank_free[n] is not None:
            wait("t", *bank_free[n])
        p = t_(TE.matmul_mx(bank[:, 0:e - m], T.wq[:, w:w + 128], T.wp[:, w:w + 128],
                            T.lc[:, CAP + m:CAP + e], T.lp[:, CAP + m:CAP + e], True, True))
        wait("s", "st", p)
        w0 = PW * (8 * o + h)
        bank_free[n] = ("ss", s_(S.activation(T.pw[:, w0 + b:w0 + e], bank[:, b - m:e - m], COPY)))
        return bank_free[n][1]

    wait("t", "sv", c_hq)
    for blocks, n in EARLY:
        for s in turn[N - blocks:]:
            wait("t", "rc%d" % s, 2 * ne)
        for k in range(*n):
            product(k // 8, k % 8, CAP * blocks)
    for s in turn:
        wait("t", "rc%d" % s, 2 * ne)

    items = [(int(o), TILES[:n].count(o)) for n, o in enumerate(TILES)]
    last, aside, pending, stores = {}, [], [], {"da": 0, "dy": 0}

    def add_to_y(o, src, ready):
        wait("g", *ready)
        wait("g", "dt%d" % o, 16)
        g.dma_start(T.y[:, 256 * o:256 * o + 256], src, accum_op=ADD).then_inc(T.sem.da, 16)
        stores["da"] += 16

    def by_scalar():
        o, h, c = pending.pop()
        win = T.pw[:, PW * (8 * o + h):PW * (8 * o + h + 1)]
        wait("s", "ss", c)
        wait("s", "sv", c_lst)
        out = T.side[:, 256 * len(aside):256 * len(aside) + 256] if h else T.acc[:, 256 * o:256 * o + 256]
        a = ("ss", s_(S.activation(out, win.indirect(T.lst[:, 16 * h:16 * h + 16]), COPY)))
        if h == 0:
            last[o] = [a, a]
        else:
            wait("y", *a)
            Y.dma_start(T.y[:, 256 * o:256 * o + 256], out).then_inc(T.sem["dt%d" % o], 16)
            aside.append(o)

    for n, (o, h) in enumerate(items):
        c = product(o, h, PW)
        if pending:
            by_scalar()
        if (o, h) in BY_SCALAR:
            pending.append((o, h, c))
            continue
        win = T.pw[:, PW * (8 * o + h):PW * (8 * o + h + 1)]
        wait("v", "ss", c)
        vw(c_lst)
        final = all(x in BY_SCALAR or x[0] != o for x in items[n + 1:])
        m = 8 if n >= HALVES else 16
        for f in range(16 // m):
            acc = T.acc[:, 256 * o + 128 * f:256 * o + 128 * f + 16 * m]
            picked = win.indirect(T.lst[:, 16 * h + 8 * f:16 * h + 8 * f + m])
            if o in last:
                wait("v", *last[o][f])
                a = ("sv", tt(acc, picked, acc, ADD))
            else:
                a = ("sv", copy(acc, picked))
            last[o] = [a, a] if m == 16 else ([a, last[o][1]] if f == 0 else [last[o][0], a])
            if final and o in aside:
                add_to_y(o, acc, a)
            elif final:
                wait("y", *a)
                Y.dma_start(T.y[:, 256 * o + 128 * f:256 * o + 128 * f + 16 * m], acc).then_inc(T.sem.dy, 16)
                stores["dy"] += 16

    wait("y", "dy", stores["dy"])
    wait("y", "dn", 128)
    wait("g", "da", stores["da"])
    wait("g", "ls", 3 * ne)
    for sem in ("sv", "ss", "st", "sg"):
        wait("g", sem, count[sem])
